import numpy as np
import ml_dtypes


def mxq(x, axis, fmt="e4m3"):
    dtype, down = {"e4m3": (ml_dtypes.float8_e4m3fn, 7), "e5m2": (ml_dtypes.float8_e5m2, 14)}[fmt]
    v = np.moveaxis(np.asarray(x, np.float32).astype(ml_dtypes.bfloat16).astype(np.float64), axis, -1)
    blocks = v.reshape(v.shape[:-1] + (-1, 32))
    amax = np.abs(blocks).max(-1, keepdims=True)
    byte = np.maximum(np.where(amax > 0, np.frexp(amax)[1] - 1 + 127, 0) - down, 1)
    scale = np.exp2(byte - 127.0)
    codes = (blocks / scale).astype(np.float32).astype(dtype).astype(np.float64)
    return np.moveaxis((codes * scale).reshape(v.shape), -1, axis)


WIDE = False


def mx_kscale(k):
    if not WIDE:
        return np.ones(k)
    levels = np.array([10, -10, 5, -5, 0])
    if k % 512:
        return np.exp2(np.random.permutation(np.resize(levels, k // 32))).repeat(32)
    a = np.empty((k // 512, 16))
    for p in range(k // 512):
        a[p, :8] = np.random.permutation(np.resize(levels, 8))
        for g in range(8):
            far = levels[np.abs(levels - a[p, g]) >= 10]
            a[p, g + 8] = far[np.random.randint(len(far))]
    return np.exp2(a.ravel()).repeat(32)


BF16 = ml_dtypes.bfloat16


def bf(x):
    return np.asarray(x, np.float32).astype(BF16)


def f64(x):
    return np.asarray(x).astype(np.float64)


E2M1 = np.array([0.0, 0.5, 1.0, 1.5, 2.0, 3.0, 4.0, 6.0, -0.0, -0.5, -1.0, -1.5, -2.0, -3.0, -4.0, -6.0])


def pack_weight(w, fmt):
    k, n = w.shape
    w = f64(bf(w)).reshape(k // 32, 32, n)
    amax = np.abs(w).max(1)
    if fmt == "e4m3":
        byte = np.frexp(amax)[1] - 1 + 127 - 7
    else:
        mant, ex = np.frexp(amax / 6.0)
        byte = np.where(mant > 0.5, ex, ex - 1) + 127
    byte = np.clip(np.where(amax > 0, byte, 1), 1, 254)
    scaled = (w * np.exp2(127.0 - byte)[:, None, :]).reshape(k, n).astype(np.float32)
    by_word = np.ascontiguousarray(scaled.reshape(k // 512, 128, 4, n).transpose(0, 1, 3, 2))
    if fmt == "e4m3":
        words = by_word.astype(ml_dtypes.float8_e4m3fn).view(np.uint8)
    else:
        c = by_word.astype(ml_dtypes.float4_e2m1fn).view(np.uint8) & 0xF
        words = c[..., 0::2] | (c[..., 1::2] << 4)
    return np.ascontiguousarray(words), np.ascontiguousarray(byte.astype(np.uint8).reshape(k // 512, 16, n))


def unpack_weight(words, scales, fmt):
    g, p, n, _ = words.shape
    if fmt == "e4m3":
        vals = np.ascontiguousarray(words).view(ml_dtypes.float8_e4m3fn).astype(np.float64)
    else:
        nib = np.empty((g, p, n, 4), np.uint8)
        nib[..., 0::2] = words & 0xF
        nib[..., 1::2] = words >> 4
        vals = E2M1[nib]
    vals = vals * np.repeat(np.exp2(scales.astype(np.float64) - 127.0), 8, axis=1)[..., None]
    return vals.transpose(0, 1, 3, 2).reshape(g * 512, n)
def pack4(w):
    words, scales = pack_weight(w, "e2m1")
    return words.reshape(words.shape[0], 128, -1), scales


def unpack4(words, scales):
    return unpack_weight(words.reshape(words.shape[0], 128, -1, 2), scales, "e2m1")


def planes(Y):
    n, m = Y.shape
    b = f64(bf(Y)).reshape(n // 32, 32, m)
    amax = np.abs(b).max(1)
    byte = np.clip(np.where(amax > 0, np.frexp(amax)[1] - 1 + 127 - 7, 1), 1, 254)
    codes = (b * np.exp2(127.0 - byte)[:, None, :]).reshape(n, m).astype(np.float32).astype(ml_dtypes.float8_e4m3fn).view(np.uint8)
    words = codes.reshape(n // 512, 128, 4, m).transpose(0, 1, 3, 2)
    return np.ascontiguousarray(words), np.ascontiguousarray(byte.astype(np.uint8).reshape(n // 512, 16, m))


P, K, F, C = 1536, 512, 2048, 1024

def setup_inputs():
    s = mx_kscale(K)
    t = mx_kscale(F)
    orient = np.random.randn(K, P) * s[:, None]
    lights = np.random.randn(K, F) / np.sqrt(K) / s[:, None] * t[None, :]
    orient_words, orient_scales = pack4(orient)
    light_words, light_scales = pack4(lights)
    albedo = 1.0 / (1.0 + np.exp(-np.random.randn(P, F)))
    sensor = 2.0 * np.random.randn(F, C) / np.sqrt(F) / t[:, None]
    falloff = np.exp(-0.5 * np.abs(np.random.randn(P)))
    dark = 0.3 * np.random.randn(C)
    gain = np.exp(0.8 * np.random.randn(C))
    return {"orient_words": orient_words, "orient_scales": orient_scales,
            "light_words": light_words, "light_scales": light_scales,
            "albedo": bf(albedo), "sensor": bf(sensor), "falloff": bf(falloff),
            "dark": bf(dark), "gain": bf(gain)}

def reference(orient_words, orient_scales, light_words, light_scales, albedo, sensor, falloff, dark, gain):
    O = unpack4(orient_words, orient_scales)
    L = unpack4(light_words, light_scales)
    shade = np.maximum(O.T @ L, 0.0)
    E = shade * f64(albedo)
    Z = mxq(E, 1, "e4m3") @ mxq(f64(sensor), 0, "e4m3")
    y = f64(gain)[None, :] * (f64(falloff)[:, None] * Z + f64(dark)[None, :])
    Y = y.T
    words, scales = planes(Y)
    return y, words, scales

@@ -1,0 +1,334 @@
+from contextlib import ExitStack
+
+import concourse.mybir as mybir
+from concourse.masks import make_identity
+
+PIXELS, CODE, LIGHTS, CHANNELS = 1536, 512, 2048, 1024
+FLOPS = 2 * PIXELS * LIGHTS * CODE + 2 * PIXELS * CHANNELS * LIGHTS
+
+F32 = mybir.dt.float32
+BF16 = mybir.dt.bfloat16
+I32 = mybir.dt.int32
+U32 = mybir.dt.uint32
+U8 = mybir.dt.uint8
+FP8X4 = mybir.dt.float8_e4m3fn_x4
+FP4X4 = mybir.dt.float4_e2m1fn_x4
+ALU = mybir.AluOpType
+
+P = 128
+BANK = 512
+TILES = PIXELS // P
+PASSES = LIGHTS // BANK
+HALVES = CHANNELS // BANK
+LAG = 2
+SCALE_SPLIT = 8
+SCALAR_COLS = 256
+
+
+def tile_photometric_sensor_render_k5_kernel(
+    tc, orient_words, orient_scales, light_words, light_scales, albedo, sensor, falloff, dark, gain,
+    out_0, out_1, out_2,
+):
+    nc = tc.nc
+    with ExitStack() as ctx:
+        keep = ctx.enter_context(tc.tile_pool(name="keep", bufs=1))
+        work = ctx.enter_context(tc.tile_pool(name="work", bufs=2))
+        psum = ctx.enter_context(tc.psum_pool(name="psum", bufs=1))
+        ctx.enter_context(tc.manual_schedule())
+
+        o_words = keep.tile([P, 2 * PIXELS], U8, align_bytes=64)
+        o_scales = keep.tile([P, PIXELS], U8, align_bytes=64)
+        l_words = keep.tile([P, 2 * LIGHTS], U8, align_bytes=64)
+        l_scales = keep.tile([P, LIGHTS], U8, align_bytes=64)
+        falloff_rows = keep.tile([P, P], BF16)
+        nc.vector.memset(o_scales[:].bitcast(I32), 0)
+        nc.vector.memset(l_scales[:].bitcast(I32), 0)
+        nc.vector.memset(falloff_rows[:], 0.0)
+
+        nc.sync.dma_start(out=l_words[:].bitcast(I32), in_=light_words[0].bitcast(I32))
+        nc.scalar.dma_start(out=o_words[:].bitcast(I32), in_=orient_words[0].bitcast(I32))
+        for q in range(4):
+            (nc.gpsimd if q < 2 else nc.scalar).dma_start(
+                out=o_scales[32 * q : 32 * q + 4, :].bitcast(I32),
+                in_=orient_scales[0, 4 * q : 4 * q + 4, :].bitcast(I32),
+            )
+            nc.sync.dma_start(
+                out=l_scales[32 * q : 32 * q + 4, :].bitcast(I32),
+                in_=light_scales[0, 4 * q : 4 * q + 4, :].bitcast(I32),
+            )
+        identity = keep.tile([P, P], F32)
+        make_identity(nc, identity[:])
+        gain_cols = keep.tile([P, CHANNELS // P], BF16)
+        dark_cols = keep.tile([P, CHANNELS // P], BF16)
+        nc.gpsimd.dma_start(out=falloff_rows[0:TILES, :], in_=falloff.rearrange("(i p) -> i p", p=P))
+        nc.gpsimd.dma_start(out=dark_cols[:], in_=dark.rearrange("(p j) -> p j", p=P))
+        nc.gpsimd.dma_start(out=gain_cols[:], in_=gain.rearrange("(p j) -> p j", p=P))
+
+        albedo_sb = {}
+        sensor_raw = {}
+
+        def load_albedo(i):
+            albedo_sb[i] = keep.tile([P, LIGHTS], BF16, name="albedo_%d" % i)
+            nc.sync.dma_start(out=albedo_sb[i][:], in_=albedo[P * i : P * (i + 1), :])
+
+        def load_sensor(h, g):
+            sensor_raw[h, g] = keep.tile([P, 4, BANK], BF16, name="sensor_raw_%d_%d" % (h, g))
+            rows = sensor[BANK * g : BANK * (g + 1), BANK * h : BANK * (h + 1)]
+            nc.sync.dma_start(out=sensor_raw[h, g][:], in_=rows.rearrange("(p t) c -> p t c", t=4))
+
+        load_albedo(0)
+        load_sensor(0, 0)
+        load_albedo(1)
+        for g in range(1, PASSES):
+            load_sensor(0, g)
+        load_albedo(2)
+        load_sensor(1, 0)
+        load_sensor(1, 1)
+        load_albedo(3)
+        load_sensor(1, 2)
+        load_sensor(1, 3)
+        for i in range(4, TILES):
+            load_albedo(i)
+
+        y_codes = [keep.tile([P, PIXELS], U32, name="y_codes_%d" % h, align_bytes=64) for h in range(HALVES)]
+        scale_parts = [(0, SCALE_SPLIT), (SCALE_SPLIT, TILES)]
+        y_scales = [
+            keep.tile([P, HALVES, P * (b - a)], U8, name="y_scales_%d" % a, align_bytes=64) for a, b in scale_parts
+        ]
+        falloff_col = keep.tile([P, TILES], F32)
+        gain_all = keep.tile([P, CHANNELS], BF16)
+        dark_all = keep.tile([P, CHANNELS], BF16)
+
+        shade = {}
+        e_pairs = {}
+        e_turned = {}
+        e_grouped = {}
+        e_codes = {}
+        e_scales = {}
+        sensor_grouped = {}
+        sensor_codes = {}
+        sensor_scales = {}
+        z = {}
+        inner = {}
+        y = {}
+        y_pairs = {}
+        y_grouped = {}
+
+        def spread_vector(cols, spread, tag, bufs):
+            bank = psum.tile([P, BANK], F32, name="spread_bank", tag=tag, bufs=bufs)
+            words = cols[:].bitcast(F32)
+            for j in range(4):
+                nc.tensor.transpose(bank[:, P * j : P * (j + 1)], words[:, j : j + 1].to_broadcast([P, P]), identity[:])
+            nc.scalar.copy(
+                out=spread[:].bitcast(F32).rearrange("q (p j) -> q p j", j=4),
+                in_=bank[:].rearrange("q (j p) -> q p j", j=4),
+            )
+
+        def prepare_vectors():
+            falloff_f32 = keep.tile([P, P], F32)
+            nc.scalar.copy(out=falloff_f32[:], in_=falloff_rows[:])
+            spread_vector(dark_cols, dark_all, "z", 2)
+            spread_vector(gain_cols, gain_all, "z", 2)
+            bank = psum.tile([P, BANK], F32, name="falloff_bank", tag="turn_y", bufs=1)
+            nc.tensor.transpose(bank[:, 0:P], falloff_f32[:], identity[:])
+            nc.scalar.copy(out=falloff_col[:], in_=bank[:, 0:TILES])
+
+        def shade_matmul(i, g):
+            shade[i, g] = psum.tile([P, BANK], F32, name="shade", tag="shade", bufs=3)
+            nc.tensor.matmul_mx(
+                out=shade[i, g][:],
+                lhsT=o_words[:, 2 * P * i : 2 * P * (i + 1)].bitcast(FP4X4),
+                lhsT_scale=o_scales[:, P * i : P * (i + 1)],
+                rhs=l_words[:, 2 * BANK * g : 2 * BANK * (g + 1)].bitcast(FP4X4),
+                rhs_scale=l_scales[:, BANK * g : BANK * (g + 1)],
+                start=True,
+                stop=True,
+            )
+
+        def reflect(i, g):
+            e_pairs[i, g] = work.tile([P, BANK], BF16, name="e_pairs", tag="e_pairs", bufs=2 * PASSES)
+            shade_v = shade[i, g][:].rearrange("p (q u e) -> p u q e", u=2, e=2)
+            albedo_v = albedo_sb[i][:, BANK * g : BANK * (g + 1)].rearrange("p (q u e) -> p u q e", u=2, e=2)
+            e_v = e_pairs[i, g][:].rearrange("p (u q e) -> p u q e", u=2, e=2)
+            for u in range(2):
+                nc.vector.scalar_tensor_tensor(
+                    out=e_v[:, u], in0=shade_v[:, u], scalar=0.0, in1=albedo_v[:, u], op0=ALU.max, op1=ALU.mult
+                )
+
+        def turn_e(i):
+            for pair in range(PASSES // 2):
+                e_turned[i, pair] = psum.tile([P, BANK], F32, name="e_turned", tag="turn_e", bufs=2)
+                for s in range(2):
+                    words = e_pairs[i, 2 * pair + s][:].bitcast(F32)
+                    for u in range(2):
+                        at = P * (2 * s + u)
+                        nc.tensor.transpose(
+                            e_turned[i, pair][:, at : at + P], words[:, P * u : P * (u + 1)], identity[:]
+                        )
+
+        def group_e(i):
+            e_grouped[i] = work.tile([P, LIGHTS], BF16, name="e_grouped", tag="e_grouped", bufs=2, align_bytes=64)
+            words = e_grouped[i][:].bitcast(F32)
+            for pair in range(PASSES // 2):
+                nc.scalar.copy(
+                    out=words[:, BANK * pair : BANK * (pair + 1)].rearrange("p (s n u) -> p s n u", s=2, u=2),
+                    in_=e_turned[i, pair][:].rearrange("p (s u n) -> p s n u", s=2, u=2),
+                )
+
+        def quantize_e(i):
+            e_codes[i] = work.tile([P, PASSES * P], U32, name="e_codes", tag="e_codes", bufs=5, align_bytes=64)
+            e_scales[i] = work.tile([P, PASSES * P], U8, name="e_scales", tag="e_scales", bufs=5, align_bytes=64)
+            nc.vector.quantize_mx(out=e_codes[i][:].bitcast(FP8X4), scales=e_scales[i][:], in_=e_grouped[i][:])
+
+        def group_sensor(h, g):
+            grouped = work.tile([P, 4 * BANK], BF16, name="sensor_grouped", tag="sensor_grouped", bufs=3, align_bytes=64)
+            sensor_grouped[h, g] = grouped
+            raw = sensor_raw[h, g]
+            nc.scalar.copy(
+                out=grouped[:, 0 : 4 * SCALAR_COLS].rearrange("p (c i t) -> p c t i", i=4, t=4),
+                in_=raw[:, :, 0:SCALAR_COLS].rearrange("p t (c i) -> p c t i", i=4),
+            )
+            nc.gpsimd.tensor_scalar(
+                out=grouped[:, 4 * SCALAR_COLS :].rearrange("p (c t) -> p c t", t=4),
+                in0=raw[:, :, SCALAR_COLS:].rearrange("p t c -> p c t"),
+                scalar1=1.0, scalar2=0.0, op0=ALU.mult, op1=ALU.add,
+            )
+
+        def quantize_sensor(h, g):
+            sensor_codes[h, g] = keep.tile([P, BANK], U32, name="sensor_codes_%d_%d" % (h, g), align_bytes=64)
+            sensor_scales[h, g] = keep.tile([P, BANK], U8, name="sensor_scales_%d_%d" % (h, g), align_bytes=64)
+            nc.vector.quantize_mx(
+                out=sensor_codes[h, g][:].bitcast(FP8X4), scales=sensor_scales[h, g][:], in_=sensor_grouped[h, g][:]
+            )
+
+        def mix_matmul(i, h):
+            z[i, h] = psum.tile([P, BANK], F32, name="z", tag="z", bufs=2)
+            for g in range(PASSES):
+                nc.tensor.matmul_mx(
+                    out=z[i, h][:],
+                    lhsT=e_codes[i][:, P * g : P * (g + 1)].bitcast(FP8X4),
+                    lhsT_scale=e_scales[i][:, P * g : P * (g + 1)],
+                    rhs=sensor_codes[h, g][:].bitcast(FP8X4),
+                    rhs_scale=sensor_scales[h, g][:],
+                    start=(g == 0),
+                    stop=(g == PASSES - 1),
+                )
+
+        def fall_and_dark(i, h):
+            inner[i, h] = work.tile([P, BANK], F32, name="inner", tag="inner", bufs=4)
+            nc.vector.scalar_tensor_tensor(
+                out=inner[i, h][:], in0=z[i, h][:], scalar=falloff_col[:, i : i + 1],
+                in1=dark_all[:, BANK * h : BANK * (h + 1)], op0=ALU.mult, op1=ALU.add,
+            )
+
+        def apply_gain(i, h):
+            y[i, h] = work.tile([P, BANK], F32, name="y", tag="y", bufs=10)
+            nc.gpsimd.tensor_tensor(
+                out=y[i, h][:], in0=inner[i, h][:], in1=gain_all[:, BANK * h : BANK * (h + 1)], op=ALU.mult
+            )
+            nc.sync.dma_start(out=out_0[P * i : P * (i + 1), BANK * h : BANK * (h + 1)], in_=y[i, h][:])
+
+        def round_y(i, h):
+            y_pairs[i, h] = work.tile([P, BANK], BF16, name="y_pairs", tag="y_pairs", bufs=4)
+            nc.scalar.copy(
+                out=y_pairs[i, h][:].rearrange("p (u q e) -> p u q e", u=2, e=2),
+                in_=y[i, h][:].rearrange("p (q u e) -> p u q e", u=2, e=2),
+            )
+
+        def turn_y(units):
+            bank = psum.tile([P, BANK], F32, name="y_turned", tag="turn_y", bufs=1)
+            for s, unit in enumerate(units):
+                words = y_pairs[unit][:].bitcast(F32)
+                for u in range(2):
+                    at = P * (2 * s + u)
+                    nc.tensor.transpose(bank[:, at : at + P], words[:, P * u : P * (u + 1)], identity[:])
+            return bank
+
+        def group_y(units, bank):
+            grouped = work.tile([P, 2 * BANK], BF16, name="y_grouped", tag="y_grouped", bufs=2, align_bytes=64)
+            width = 2 * P * len(units)
+            nc.scalar.copy(
+                out=grouped[:].bitcast(F32)[:, 0:width].rearrange("p (s n u) -> p s n u", n=P, u=2),
+                in_=bank[:, 0:width].rearrange("p (s u n) -> p s n u", n=P, u=2),
+            )
+            for s, unit in enumerate(units):
+                y_grouped[unit] = grouped[:, BANK * s : BANK * (s + 1)]
+
+        def quantize_y(i, h):
+            part = 0 if i < SCALE_SPLIT else 1
+            at = P * (i - scale_parts[part][0])
+            nc.vector.quantize_mx(
+                out=y_codes[h][:, P * i : P * (i + 1)].bitcast(FP8X4),
+                scales=y_scales[part][:, h, at : at + P],
+                in_=y_grouped[i, h],
+            )
+            if i % 2 == 1:
+                m0, m1 = P * (i - 1), P * (i + 1)
+                nc.sync.dma_start(
+                    out=out_1[h].rearrange("p m t -> p (m t)")[:, 4 * m0 : 4 * m1].bitcast(I32),
+                    in_=y_codes[h][:, m0:m1].bitcast(I32),
+                )
+            if h == HALVES - 1 and i == scale_parts[part][1] - 1:
+                m0, m1 = P * scale_parts[part][0], P * scale_parts[part][1]
+                for q in range(4):
+                    nc.sync.dma_start(
+                        out=out_2[:, 4 * q : 4 * q + 4, m0:m1].rearrange("h r m -> r h m").bitcast(I32),
+                        in_=y_scales[part][32 * q : 32 * q + 4].bitcast(I32),
+                    )
+
+        order = [(i, 0) for i in range(LAG)]
+        for i in range(LAG, TILES):
+            order.extend([(i, 0), (i - LAG, 1)])
+        order.extend([(i, 1) for i in range(TILES - LAG, TILES)])
+        mix_at = {2 + s: [order[s]] for s in range(LAG)}
+        for s in range((len(order) - LAG) // 2):
+            mix_at[2 + LAG + s] = order[LAG + 2 * s : LAG + 2 * s + 2]
+        sensor_at = {0: [(0, 0)], 1: [(0, 1), (0, 2), (0, 3)], 2: [(1, 0), (1, 1)], 3: [(1, 2), (1, 3)]}
+
+        for g in range(3):
+            shade_matmul(0, g)
+
+        for step in range(max(mix_at) + 3):
+            mixing = mix_at.get(step, [])
+            finishing = mix_at.get(step - 1, [])
+            leaving = mix_at.get(step - 2, [])
+            shading = step < TILES
+            turning = 1 <= step <= TILES
+
+            if turning:
+                turn_e(step - 1)
+            if leaving:
+                y_bank = turn_y(leaving)
+            for unit in finishing:
+                fall_and_dark(*unit)
+            if turning:
+                group_e(step - 1)
+            if leaving:
+                group_y(leaving, y_bank)
+            if step == 1:
+                prepare_vectors()
+            for unit in finishing:
+                apply_gain(*unit)
+            for piece in sensor_at.get(step, []):
+                group_sensor(*piece)
+            for unit in finishing:
+                round_y(*unit)
+
+            if mixing:
+                mix_matmul(*mixing[0])
+            if shading:
+                reflect(step, 0)
+                shade_matmul(step, 3)
+            if len(mixing) > 1:
+                mix_matmul(*mixing[1])
+            if shading:
+                for g in range(1, PASSES):
+                    reflect(step, g)
+                    if step + 1 < TILES:
+                        shade_matmul(step + 1, g - 1)
+            if turning:
+                quantize_e(step - 1)
+            for piece in sensor_at.get(step, []):
+                quantize_sensor(*piece)
+            for unit in leaving:
+                quantize_y(*unit)

@@ -21,7 +21,7 @@ TILES = PIXELS // P
 PASSES = LIGHTS // BANK
 HALVES = CHANNELS // BANK
 LAG = 2
-SCALE_SPLIT = 8
+SCALE_SPLIT = 6
 SCALAR_COLS = 256
 
 
@@ -48,7 +48,7 @@ def tile_photometric_sensor_render_k5_kernel(
         nc.sync.dma_start(out=l_words[:].bitcast(I32), in_=light_words[0].bitcast(I32))
         nc.scalar.dma_start(out=o_words[:].bitcast(I32), in_=orient_words[0].bitcast(I32))
         for q in range(4):
-            (nc.gpsimd if q < 2 else nc.scalar).dma_start(
+            (nc.gpsimd if q < 3 else nc.scalar).dma_start(
                 out=o_scales[32 * q : 32 * q + 4, :].bitcast(I32),
                 in_=orient_scales[0, 4 * q : 4 * q + 4, :].bitcast(I32),
             )
@@ -77,16 +77,15 @@ def tile_photometric_sensor_render_k5_kernel(
             nc.sync.dma_start(out=sensor_raw[h, g][:], in_=rows.rearrange("(p t) c -> p t c", t=4))
 
         load_albedo(0)
-        load_sensor(0, 0)
-        load_albedo(1)
-        for g in range(1, PASSES):
-            load_sensor(0, g)
-        load_albedo(2)
-        load_sensor(1, 0)
-        load_sensor(1, 1)
-        load_albedo(3)
-        load_sensor(1, 2)
-        load_sensor(1, 3)
+        for h in range(HALVES):
+            load_sensor(h, 0)
+            if h == 1:
+                load_sensor(h, 1)
+            load_albedo(1 + 2 * h)
+            for g in range(1 + h, PASSES):
+                load_sensor(h, g)
+            if h == 0:
+                load_albedo(2)
         for i in range(4, TILES):
             load_albedo(i)
 
@@ -180,29 +179,35 @@ def tile_photometric_sensor_render_k5_kernel(
             e_scales[i] = work.tile([P, PASSES * P], U8, name="e_scales", tag="e_scales", bufs=5, align_bytes=64)
             nc.vector.quantize_mx(out=e_codes[i][:].bitcast(FP8X4), scales=e_scales[i][:], in_=e_grouped[i][:])
 
-        def group_sensor(h, g):
-            grouped = work.tile([P, 4 * BANK], BF16, name="sensor_grouped", tag="sensor_grouped", bufs=3, align_bytes=64)
-            sensor_grouped[h, g] = grouped
-            raw = sensor_raw[h, g]
-            nc.scalar.copy(
-                out=grouped[:, 0 : 4 * SCALAR_COLS].rearrange("p (c i t) -> p c t i", i=4, t=4),
-                in_=raw[:, :, 0:SCALAR_COLS].rearrange("p t (c i) -> p c t i", i=4),
-            )
-            nc.gpsimd.tensor_scalar(
-                out=grouped[:, 4 * SCALAR_COLS :].rearrange("p (c t) -> p c t", t=4),
-                in0=raw[:, :, SCALAR_COLS:].rearrange("p t c -> p c t"),
-                scalar1=1.0, scalar2=0.0, op0=ALU.mult, op1=ALU.add,
-            )
+        def group_sensor(h, g, side, engine):
+            grouped = work.tile([P, 2 * BANK], BF16, name="sensor_grouped", tag="sensor_grouped", bufs=6, align_bytes=64)
+            sensor_grouped[h, g, side] = grouped
+            raw = sensor_raw[h, g][:, :, side * BANK // 2 : (side + 1) * BANK // 2]
+            if engine == "g":
+                nc.gpsimd.tensor_scalar(
+                    out=grouped[:].rearrange("p (c t) -> p c t", t=4),
+                    in0=raw.rearrange("p t c -> p c t"),
+                    scalar1=1.0, scalar2=0.0, op0=ALU.mult, op1=ALU.add,
+                )
+            else:
+                (nc.scalar.copy if engine == "s" else nc.vector.tensor_copy)(
+                    out=grouped[:].rearrange("p (c i t) -> p c t i", i=4, t=4),
+                    in_=raw.rearrange("p t (c i) -> p c t i", i=4),
+                )
 
         def quantize_sensor(h, g):
             sensor_codes[h, g] = keep.tile([P, BANK], U32, name="sensor_codes_%d_%d" % (h, g), align_bytes=64)
             sensor_scales[h, g] = keep.tile([P, BANK], U8, name="sensor_scales_%d_%d" % (h, g), align_bytes=64)
-            nc.vector.quantize_mx(
-                out=sensor_codes[h, g][:].bitcast(FP8X4), scales=sensor_scales[h, g][:], in_=sensor_grouped[h, g][:]
-            )
+            for side in range(2):
+                cols = slice(side * BANK // 2, (side + 1) * BANK // 2)
+                nc.vector.quantize_mx(
+                    out=sensor_codes[h, g][:, cols].bitcast(FP8X4),
+                    scales=sensor_scales[h, g][:, cols],
+                    in_=sensor_grouped[h, g, side][:],
+                )
 
-        def mix_matmul(i, h):
-            z[i, h] = psum.tile([P, BANK], F32, name="z", tag="z", bufs=2)
+        def mix_matmul(i, h, tag="z", bufs=2):
+            z[i, h] = psum.tile([P, BANK], F32, name="z", tag=tag, bufs=bufs)
             for g in range(PASSES):
                 nc.tensor.matmul_mx(
                     out=z[i, h][:],
@@ -215,28 +220,28 @@ def tile_photometric_sensor_render_k5_kernel(
                 )
 
         def fall_and_dark(i, h):
-            inner[i, h] = work.tile([P, BANK], F32, name="inner", tag="inner", bufs=4)
+            inner[i, h] = work.tile([P, BANK], F32, name="inner", tag="inner", bufs=6)
             nc.vector.scalar_tensor_tensor(
                 out=inner[i, h][:], in0=z[i, h][:], scalar=falloff_col[:, i : i + 1],
                 in1=dark_all[:, BANK * h : BANK * (h + 1)], op0=ALU.mult, op1=ALU.add,
             )
 
-        def apply_gain(i, h):
+        def apply_gain(i, h, engine=nc.gpsimd):
             y[i, h] = work.tile([P, BANK], F32, name="y", tag="y", bufs=10)
-            nc.gpsimd.tensor_tensor(
+            engine.tensor_tensor(
                 out=y[i, h][:], in0=inner[i, h][:], in1=gain_all[:, BANK * h : BANK * (h + 1)], op=ALU.mult
             )
             nc.sync.dma_start(out=out_0[P * i : P * (i + 1), BANK * h : BANK * (h + 1)], in_=y[i, h][:])
 
         def round_y(i, h):
-            y_pairs[i, h] = work.tile([P, BANK], BF16, name="y_pairs", tag="y_pairs", bufs=4)
+            y_pairs[i, h] = work.tile([P, BANK], BF16, name="y_pairs", tag="y_pairs", bufs=6)
             nc.scalar.copy(
                 out=y_pairs[i, h][:].rearrange("p (u q e) -> p u q e", u=2, e=2),
                 in_=y[i, h][:].rearrange("p (q u e) -> p u q e", u=2, e=2),
             )
 
-        def turn_y(units):
-            bank = psum.tile([P, BANK], F32, name="y_turned", tag="turn_y", bufs=1)
+        def turn_y(units, tag="turn_y", bufs=1):
+            bank = psum.tile([P, BANK], F32, name="y_turned", tag=tag, bufs=bufs)
             for s, unit in enumerate(units):
                 words = y_pairs[unit][:].bitcast(F32)
                 for u in range(2):
@@ -245,7 +250,7 @@ def tile_photometric_sensor_render_k5_kernel(
             return bank
 
         def group_y(units, bank):
-            grouped = work.tile([P, 2 * BANK], BF16, name="y_grouped", tag="y_grouped", bufs=2, align_bytes=64)
+            grouped = work.tile([P, 2 * BANK], BF16, name="y_grouped", tag="y_grouped", bufs=4, align_bytes=64)
             width = 2 * P * len(units)
             nc.scalar.copy(
                 out=grouped[:].bitcast(F32)[:, 0:width].rearrange("p (s n u) -> p s n u", n=P, u=2),
@@ -276,59 +281,119 @@ def tile_photometric_sensor_render_k5_kernel(
                         in_=y_scales[part][32 * q : 32 * q + 4].bitcast(I32),
                     )
 
-        order = [(i, 0) for i in range(LAG)]
-        for i in range(LAG, TILES):
-            order.extend([(i, 0), (i - LAG, 1)])
-        order.extend([(i, 1) for i in range(TILES - LAG, TILES)])
-        mix_at = {2 + s: [order[s]] for s in range(LAG)}
-        for s in range((len(order) - LAG) // 2):
-            mix_at[2 + LAG + s] = order[LAG + 2 * s : LAG + 2 * s + 2]
-        sensor_at = {0: [(0, 0)], 1: [(0, 1), (0, 2), (0, 3)], 2: [(1, 0), (1, 1)], 3: [(1, 2), (1, 3)]}
+        def mixed_in(step):
+            return [(i, h) for i, h in ((step - 2, 0), (step - 2 - LAG, 1)) if 0 <= i]
 
         for g in range(3):
             shade_matmul(0, g)
 
-        for step in range(max(mix_at) + 3):
-            mixing = mix_at.get(step, [])
-            finishing = mix_at.get(step - 1, [])
-            leaving = mix_at.get(step - 2, [])
-            shading = step < TILES
-            turning = 1 <= step <= TILES
+        for step in range(TILES):
+            mixing = mixed_in(step)
+            finishing = mixed_in(step - 1)
+            leaving = mixed_in(step - 2)
+            opening = step // 2 if step % 2 == 0 and step // 2 < HALVES else None
+            middle = step // 2 if step % 2 == 1 and step // 2 < HALVES else None
+            closing = step // 2 - 1 if step % 2 == 0 and 1 <= step // 2 <= HALVES else None
 
-            if turning:
+            if step >= 1:
                 turn_e(step - 1)
             if leaving:
                 y_bank = turn_y(leaving)
             for unit in finishing:
                 fall_and_dark(*unit)
-            if turning:
+            if closing is not None:
+                group_sensor(closing, 3, 1, "g")
+            if middle is not None:
+                group_sensor(middle, 1, 1, "g")
+            if middle == 0:
+                group_sensor(middle, 2, 1, "g")
+                group_sensor(middle, 1, 0, "s")
+            if step >= 1:
                 group_e(step - 1)
             if leaving:
                 group_y(leaving, y_bank)
-            if step == 1:
+            if step == 2:
                 prepare_vectors()
             for unit in finishing:
                 apply_gain(*unit)
-            for piece in sensor_at.get(step, []):
-                group_sensor(*piece)
+            if opening is not None:
+                group_sensor(opening, 0, 1, "g")
+                group_sensor(opening, 0, 0, "s")
+            if opening == 1:
+                group_sensor(opening, 1, 0, "s")
+            if middle == 1:
+                group_sensor(middle, 2, 1, "g")
+            if middle is not None:
+                group_sensor(middle, 2, 0, "s")
+                group_sensor(middle, 3, 0, "s")
             for unit in finishing:
                 round_y(*unit)
 
-            if mixing:
-                mix_matmul(*mixing[0])
-            if shading:
-                reflect(step, 0)
-                shade_matmul(step, 3)
             if len(mixing) > 1:
-                mix_matmul(*mixing[1])
-            if shading:
-                for g in range(1, PASSES):
-                    reflect(step, g)
-                    if step + 1 < TILES:
-                        shade_matmul(step + 1, g - 1)
-            if turning:
+                mix_matmul(*mixing[0])
+            reflect(step, 0)
+            shade_matmul(step, 3)
+            reflect(step, 1)
+            if closing is not None:
+                quantize_sensor(closing, 3)
+            if mixing:
+                mix_matmul(*mixing[-1])
+            for g in range(2, PASSES):
+                reflect(step, g)
+            if step + 1 < TILES:
+                for g in range(3):
+                    shade_matmul(step + 1, g)
+            if step >= 1:
                 quantize_e(step - 1)
-            for piece in sensor_at.get(step, []):
-                quantize_sensor(*piece)
+            if opening is not None:
+                quantize_sensor(opening, 0)
+            if middle is not None:
+                quantize_sensor(middle, 1)
+                quantize_sensor(middle, 2)
             for unit in leaving:
                 quantize_y(*unit)
+
+        last = TILES - 1
+        pairs = [mixed_in(last - 1), mixed_in(last), mixed_in(last + 1)]
+        pairs.append([(last - 2, 1), (last - 1, 1)])
+        pairs.append([(last, 0), (last, 1)])
+
+        turn_e(last)
+        y_bank = turn_y(pairs[0])
+        for unit in pairs[1]:
+            fall_and_dark(*unit)
+        group_e(last)
+        group_y(pairs[0], y_bank)
+        for unit in pairs[1]:
+            apply_gain(*unit)
+            round_y(*unit)
+        for unit in pairs[2]:
+            mix_matmul(*unit)
+        for unit in pairs[3]:
+            mix_matmul(*unit, tag="shade", bufs=3)
+        for n in range(2, len(pairs)):
+            first, second = pairs[n]
+            fall_and_dark(*first)
+            if n == 2:
+                quantize_e(last)
+                for unit in pairs[0]:
+                    quantize_y(*unit)
+            fall_and_dark(*second)
+            for unit in pairs[n]:
+                apply_gain(*unit, engine=nc.gpsimd if n == 2 else nc.vector)
+            if n == 2:
+                mix_matmul(*pairs[-1][0], tag="shade", bufs=3)
+                y_bank = turn_y(pairs[n - 1])
+                mix_matmul(*pairs[-1][1])
+            else:
+                y_bank = turn_y(pairs[n - 1], "turn_e", 2)
+            round_y(*first)
+            group_y(pairs[n - 1], y_bank)
+            round_y(*second)
+            if n > 2:
+                for unit in pairs[n - 2]:
+                    quantize_y(*unit)
+        for unit, tag, bufs in zip(pairs[-1], ("turn_y", "turn_e"), (1, 2)):
+            group_y([unit], turn_y([unit], tag, bufs))
+        for unit in pairs[-2] + pairs[-1]:
+            quantize_y(*unit)

@@ -20,9 +20,16 @@ BANK = 512
 TILES = PIXELS // P
 PASSES = LIGHTS // BANK
 HALVES = CHANNELS // BANK
-LAG = 2
+SIDE = BANK // 2
+
+MIX_DELAY = 2
+HALF_LAG = 2
 SCALE_SPLIT = 6
-SCALAR_COLS = 256
+
+SHADE_BANKS = {"tag": "shade", "bufs": 3}
+Z_BANKS = {"tag": "z", "bufs": 2}
+TURN_E_BANKS = {"tag": "turn_e", "bufs": 2}
+TURN_Y_BANKS = {"tag": "turn_y", "bufs": 1}
 
 
 def tile_photometric_sensor_render_k5_kernel(
@@ -41,31 +48,21 @@ def tile_photometric_sensor_render_k5_kernel(
         l_words = keep.tile([P, 2 * LIGHTS], U8, align_bytes=64)
         l_scales = keep.tile([P, LIGHTS], U8, align_bytes=64)
         falloff_rows = keep.tile([P, P], BF16)
+        gain_cols = keep.tile([P, CHANNELS // P], BF16)
+        dark_cols = keep.tile([P, CHANNELS // P], BF16)
+        identity = keep.tile([P, P], F32)
+        albedo_sb = {}
+        sensor_raw = {}
+
         nc.vector.memset(o_scales[:].bitcast(I32), 0)
         nc.vector.memset(l_scales[:].bitcast(I32), 0)
         nc.vector.memset(falloff_rows[:], 0.0)
 
-        nc.sync.dma_start(out=l_words[:].bitcast(I32), in_=light_words[0].bitcast(I32))
-        nc.scalar.dma_start(out=o_words[:].bitcast(I32), in_=orient_words[0].bitcast(I32))
-        for q in range(4):
-            (nc.gpsimd if q < 3 else nc.scalar).dma_start(
-                out=o_scales[32 * q : 32 * q + 4, :].bitcast(I32),
-                in_=orient_scales[0, 4 * q : 4 * q + 4, :].bitcast(I32),
-            )
-            nc.sync.dma_start(
-                out=l_scales[32 * q : 32 * q + 4, :].bitcast(I32),
-                in_=light_scales[0, 4 * q : 4 * q + 4, :].bitcast(I32),
-            )
-        identity = keep.tile([P, P], F32)
-        make_identity(nc, identity[:])
-        gain_cols = keep.tile([P, CHANNELS // P], BF16)
-        dark_cols = keep.tile([P, CHANNELS // P], BF16)
-        nc.gpsimd.dma_start(out=falloff_rows[0:TILES, :], in_=falloff.rearrange("(i p) -> i p", p=P))
-        nc.gpsimd.dma_start(out=dark_cols[:], in_=dark.rearrange("(p j) -> p j", p=P))
-        nc.gpsimd.dma_start(out=gain_cols[:], in_=gain.rearrange("(p j) -> p j", p=P))
-
-        albedo_sb = {}
-        sensor_raw = {}
+        def load_scale_rows(plane, rows, quadrants, queue):
+            for q in quadrants:
+                queue.dma_start(
+                    out=plane[32 * q : 32 * q + 4, :].bitcast(I32), in_=rows[0, 4 * q : 4 * q + 4, :].bitcast(I32)
+                )
 
         def load_albedo(i):
             albedo_sb[i] = keep.tile([P, LIGHTS], BF16, name="albedo_%d" % i)
@@ -76,45 +73,60 @@ def tile_photometric_sensor_render_k5_kernel(
             rows = sensor[BANK * g : BANK * (g + 1), BANK * h : BANK * (h + 1)]
             nc.sync.dma_start(out=sensor_raw[h, g][:], in_=rows.rearrange("(p t) c -> p t c", t=4))
 
+        load_scale_rows(o_scales, orient_scales, (0, 1), nc.gpsimd)
+        make_identity(nc, identity[:])
+        nc.sync.dma_start(out=l_words[:].bitcast(I32), in_=light_words[0].bitcast(I32))
+        nc.sync.dma_start(out=o_words[:].bitcast(I32), in_=orient_words[0].bitcast(I32))
+        load_scale_rows(o_scales, orient_scales, (2, 3), nc.sync)
+        load_scale_rows(l_scales, light_scales, range(4), nc.sync)
         load_albedo(0)
-        for h in range(HALVES):
-            load_sensor(h, 0)
-            if h == 1:
-                load_sensor(h, 1)
-            load_albedo(1 + 2 * h)
-            for g in range(1 + h, PASSES):
-                load_sensor(h, g)
-            if h == 0:
-                load_albedo(2)
+        nc.sync.dma_start(out=dark_cols[:], in_=dark.rearrange("(p j) -> p j", p=P))
+        nc.sync.dma_start(out=gain_cols[:], in_=gain.rearrange("(p j) -> p j", p=P))
+        nc.sync.dma_start(out=falloff_rows[0:TILES, :], in_=falloff.rearrange("(i p) -> i p", p=P))
+        load_sensor(0, 0)
+        load_sensor(0, 1)
+        load_albedo(1)
+        load_sensor(0, 2)
+        load_sensor(0, 3)
+        load_sensor(1, 0)
+        load_albedo(2)
+        load_sensor(1, 1)
+        load_albedo(3)
+        load_sensor(1, 2)
+        load_sensor(1, 3)
         for i in range(4, TILES):
             load_albedo(i)
 
+        falloff_col = keep.tile([P, TILES], F32)
+        gain_all = keep.tile([P, CHANNELS], BF16)
+        dark_all = keep.tile([P, CHANNELS], BF16)
         y_codes = [keep.tile([P, PIXELS], U32, name="y_codes_%d" % h, align_bytes=64) for h in range(HALVES)]
         scale_parts = [(0, SCALE_SPLIT), (SCALE_SPLIT, TILES)]
         y_scales = [
             keep.tile([P, HALVES, P * (b - a)], U8, name="y_scales_%d" % a, align_bytes=64) for a, b in scale_parts
         ]
-        falloff_col = keep.tile([P, TILES], F32)
-        gain_all = keep.tile([P, CHANNELS], BF16)
-        dark_all = keep.tile([P, CHANNELS], BF16)
+        sensor_codes = {}
+        sensor_scales = {}
+        for h in range(HALVES):
+            for g in range(PASSES):
+                sensor_codes[h, g] = keep.tile([P, BANK], U32, name="sensor_codes_%d_%d" % (h, g), align_bytes=64)
+                sensor_scales[h, g] = keep.tile([P, BANK], U8, name="sensor_scales_%d_%d" % (h, g), align_bytes=64)
 
+        sensor_grouped = {}
         shade = {}
         e_pairs = {}
         e_turned = {}
         e_grouped = {}
         e_codes = {}
         e_scales = {}
-        sensor_grouped = {}
-        sensor_codes = {}
-        sensor_scales = {}
         z = {}
         inner = {}
         y = {}
         y_pairs = {}
         y_grouped = {}
 
-        def spread_vector(cols, spread, tag, bufs):
-            bank = psum.tile([P, BANK], F32, name="spread_bank", tag=tag, bufs=bufs)
+        def spread_vector(cols, spread):
+            bank = psum.tile([P, BANK], F32, name="spread_bank", **Z_BANKS)
             words = cols[:].bitcast(F32)
             for j in range(4):
                 nc.tensor.transpose(bank[:, P * j : P * (j + 1)], words[:, j : j + 1].to_broadcast([P, P]), identity[:])
@@ -126,14 +138,31 @@ def tile_photometric_sensor_render_k5_kernel(
         def prepare_vectors():
             falloff_f32 = keep.tile([P, P], F32)
             nc.scalar.copy(out=falloff_f32[:], in_=falloff_rows[:])
-            spread_vector(dark_cols, dark_all, "z", 2)
-            spread_vector(gain_cols, gain_all, "z", 2)
-            bank = psum.tile([P, BANK], F32, name="falloff_bank", tag="turn_y", bufs=1)
+            spread_vector(dark_cols, dark_all)
+            spread_vector(gain_cols, gain_all)
+            bank = psum.tile([P, BANK], F32, name="falloff_bank", **TURN_Y_BANKS)
             nc.tensor.transpose(bank[:, 0:P], falloff_f32[:], identity[:])
             nc.scalar.copy(out=falloff_col[:], in_=bank[:, 0:TILES])
 
+        def group_sensor(h, g, side, copy):
+            grouped = work.tile([P, 4 * SIDE], BF16, name="sensor_grouped", tag="sensor_grouped", bufs=8, align_bytes=64)
+            sensor_grouped[h, g, side] = grouped
+            copy(
+                out=grouped[:].rearrange("p (c i t) -> p c t i", i=4, t=4),
+                in_=sensor_raw[h, g][:, :, SIDE * side : SIDE * (side + 1)].rearrange("p t (c i) -> p c t i", i=4),
+            )
+
+        def quantize_sensor(h, g):
+            for side in range(2):
+                cols = slice(SIDE * side, SIDE * (side + 1))
+                nc.vector.quantize_mx(
+                    out=sensor_codes[h, g][:, cols].bitcast(FP8X4),
+                    scales=sensor_scales[h, g][:, cols],
+                    in_=sensor_grouped[h, g, side][:],
+                )
+
         def shade_matmul(i, g):
-            shade[i, g] = psum.tile([P, BANK], F32, name="shade", tag="shade", bufs=3)
+            shade[i, g] = psum.tile([P, BANK], F32, name="shade", **SHADE_BANKS)
             nc.tensor.matmul_mx(
                 out=shade[i, g][:],
                 lhsT=o_words[:, 2 * P * i : 2 * P * (i + 1)].bitcast(FP4X4),
@@ -146,71 +175,50 @@ def tile_photometric_sensor_render_k5_kernel(
 
         def reflect(i, g):
             e_pairs[i, g] = work.tile([P, BANK], BF16, name="e_pairs", tag="e_pairs", bufs=2 * PASSES)
-            shade_v = shade[i, g][:].rearrange("p (q u e) -> p u q e", u=2, e=2)
-            albedo_v = albedo_sb[i][:, BANK * g : BANK * (g + 1)].rearrange("p (q u e) -> p u q e", u=2, e=2)
-            e_v = e_pairs[i, g][:].rearrange("p (u q e) -> p u q e", u=2, e=2)
+            shade_v = shade[i, g][:].rearrange("n (p u e) -> n u p e", u=2, e=2)
+            albedo_v = albedo_sb[i][:, BANK * g : BANK * (g + 1)].rearrange("n (p u e) -> n u p e", u=2, e=2)
+            e_v = e_pairs[i, g][:].rearrange("n (u p e) -> n u p e", u=2, e=2)
             for u in range(2):
                 nc.vector.scalar_tensor_tensor(
                     out=e_v[:, u], in0=shade_v[:, u], scalar=0.0, in1=albedo_v[:, u], op0=ALU.max, op1=ALU.mult
                 )
 
+        def turn_words(bank, sources):
+            for s, source in enumerate(sources):
+                words = source[:].bitcast(F32)
+                for u in range(2):
+                    at = P * (2 * s + u)
+                    nc.tensor.transpose(bank[:, at : at + P], words[:, P * u : P * (u + 1)], identity[:])
+
+        def group_words(words, bank):
+            nc.scalar.copy(
+                out=words.rearrange("p (s n u) -> p s n u", n=P, u=2),
+                in_=bank.rearrange("p (s u n) -> p s n u", n=P, u=2),
+            )
+
         def turn_e(i):
             for pair in range(PASSES // 2):
-                e_turned[i, pair] = psum.tile([P, BANK], F32, name="e_turned", tag="turn_e", bufs=2)
-                for s in range(2):
-                    words = e_pairs[i, 2 * pair + s][:].bitcast(F32)
-                    for u in range(2):
-                        at = P * (2 * s + u)
-                        nc.tensor.transpose(
-                            e_turned[i, pair][:, at : at + P], words[:, P * u : P * (u + 1)], identity[:]
-                        )
+                e_turned[i, pair] = psum.tile([P, BANK], F32, name="e_turned", **TURN_E_BANKS)
+                turn_words(e_turned[i, pair], [e_pairs[i, 2 * pair], e_pairs[i, 2 * pair + 1]])
 
         def group_e(i):
             e_grouped[i] = work.tile([P, LIGHTS], BF16, name="e_grouped", tag="e_grouped", bufs=2, align_bytes=64)
             words = e_grouped[i][:].bitcast(F32)
             for pair in range(PASSES // 2):
-                nc.scalar.copy(
-                    out=words[:, BANK * pair : BANK * (pair + 1)].rearrange("p (s n u) -> p s n u", s=2, u=2),
-                    in_=e_turned[i, pair][:].rearrange("p (s u n) -> p s n u", s=2, u=2),
-                )
+                group_words(words[:, BANK * pair : BANK * (pair + 1)], e_turned[i, pair][:])
 
         def quantize_e(i):
-            e_codes[i] = work.tile([P, PASSES * P], U32, name="e_codes", tag="e_codes", bufs=5, align_bytes=64)
-            e_scales[i] = work.tile([P, PASSES * P], U8, name="e_scales", tag="e_scales", bufs=5, align_bytes=64)
+            bufs = HALF_LAG + 3
+            e_codes[i] = work.tile([P, PASSES * P], U32, name="e_codes", tag="e_codes", bufs=bufs, align_bytes=64)
+            e_scales[i] = work.tile([P, PASSES * P], U8, name="e_scales", tag="e_scales", bufs=bufs, align_bytes=64)
             nc.vector.quantize_mx(out=e_codes[i][:].bitcast(FP8X4), scales=e_scales[i][:], in_=e_grouped[i][:])
 
-        def group_sensor(h, g, side, engine):
-            grouped = work.tile([P, 2 * BANK], BF16, name="sensor_grouped", tag="sensor_grouped", bufs=6, align_bytes=64)
-            sensor_grouped[h, g, side] = grouped
-            raw = sensor_raw[h, g][:, :, side * BANK // 2 : (side + 1) * BANK // 2]
-            if engine == "g":
-                nc.gpsimd.tensor_scalar(
-                    out=grouped[:].rearrange("p (c t) -> p c t", t=4),
-                    in0=raw.rearrange("p t c -> p c t"),
-                    scalar1=1.0, scalar2=0.0, op0=ALU.mult, op1=ALU.add,
-                )
-            else:
-                (nc.scalar.copy if engine == "s" else nc.vector.tensor_copy)(
-                    out=grouped[:].rearrange("p (c i t) -> p c t i", i=4, t=4),
-                    in_=raw.rearrange("p t (c i) -> p c t i", i=4),
-                )
-
-        def quantize_sensor(h, g):
-            sensor_codes[h, g] = keep.tile([P, BANK], U32, name="sensor_codes_%d_%d" % (h, g), align_bytes=64)
-            sensor_scales[h, g] = keep.tile([P, BANK], U8, name="sensor_scales_%d_%d" % (h, g), align_bytes=64)
-            for side in range(2):
-                cols = slice(side * BANK // 2, (side + 1) * BANK // 2)
-                nc.vector.quantize_mx(
-                    out=sensor_codes[h, g][:, cols].bitcast(FP8X4),
-                    scales=sensor_scales[h, g][:, cols],
-                    in_=sensor_grouped[h, g, side][:],
-                )
-
-        def mix_matmul(i, h, tag="z", bufs=2):
-            z[i, h] = psum.tile([P, BANK], F32, name="z", tag=tag, bufs=bufs)
+        def mix_matmul(unit, banks):
+            i, h = unit
+            z[unit] = psum.tile([P, BANK], F32, name="z", **banks)
             for g in range(PASSES):
                 nc.tensor.matmul_mx(
-                    out=z[i, h][:],
+                    out=z[unit][:],
                     lhsT=e_codes[i][:, P * g : P * (g + 1)].bitcast(FP8X4),
                     lhsT_scale=e_scales[i][:, P * g : P * (g + 1)],
                     rhs=sensor_codes[h, g][:].bitcast(FP8X4),
@@ -219,53 +227,49 @@ def tile_photometric_sensor_render_k5_kernel(
                     stop=(g == PASSES - 1),
                 )
 
-        def fall_and_dark(i, h):
-            inner[i, h] = work.tile([P, BANK], F32, name="inner", tag="inner", bufs=6)
+        def fall_and_dark(unit):
+            i, h = unit
+            inner[unit] = work.tile([P, BANK], F32, name="inner", tag="inner", bufs=6)
             nc.vector.scalar_tensor_tensor(
-                out=inner[i, h][:], in0=z[i, h][:], scalar=falloff_col[:, i : i + 1],
+                out=inner[unit][:], in0=z[unit][:], scalar=falloff_col[:, i : i + 1],
                 in1=dark_all[:, BANK * h : BANK * (h + 1)], op0=ALU.mult, op1=ALU.add,
             )
 
-        def apply_gain(i, h, engine=nc.gpsimd):
-            y[i, h] = work.tile([P, BANK], F32, name="y", tag="y", bufs=10)
+        def apply_gain(unit, engine):
+            i, h = unit
+            y[unit] = work.tile([P, BANK], F32, name="y", tag="y", bufs=10)
             engine.tensor_tensor(
-                out=y[i, h][:], in0=inner[i, h][:], in1=gain_all[:, BANK * h : BANK * (h + 1)], op=ALU.mult
+                out=y[unit][:], in0=inner[unit][:], in1=gain_all[:, BANK * h : BANK * (h + 1)], op=ALU.mult
             )
-            nc.sync.dma_start(out=out_0[P * i : P * (i + 1), BANK * h : BANK * (h + 1)], in_=y[i, h][:])
+            nc.sync.dma_start(out=out_0[P * i : P * (i + 1), BANK * h : BANK * (h + 1)], in_=y[unit][:])
 
-        def round_y(i, h):
-            y_pairs[i, h] = work.tile([P, BANK], BF16, name="y_pairs", tag="y_pairs", bufs=6)
-            nc.scalar.copy(
-                out=y_pairs[i, h][:].rearrange("p (u q e) -> p u q e", u=2, e=2),
-                in_=y[i, h][:].rearrange("p (q u e) -> p u q e", u=2, e=2),
+        def round_y(unit, copy):
+            y_pairs[unit] = work.tile([P, BANK], BF16, name="y_pairs", tag="y_pairs", bufs=6)
+            copy(
+                out=y_pairs[unit][:].rearrange("n (u p e) -> n u p e", u=2, e=2),
+                in_=y[unit][:].rearrange("n (p u e) -> n u p e", u=2, e=2),
             )
 
-        def turn_y(units, tag="turn_y", bufs=1):
-            bank = psum.tile([P, BANK], F32, name="y_turned", tag=tag, bufs=bufs)
-            for s, unit in enumerate(units):
-                words = y_pairs[unit][:].bitcast(F32)
-                for u in range(2):
-                    at = P * (2 * s + u)
-                    nc.tensor.transpose(bank[:, at : at + P], words[:, P * u : P * (u + 1)], identity[:])
+        def turn_y(units, banks):
+            bank = psum.tile([P, BANK], F32, name="y_turned", **banks)
+            turn_words(bank, [y_pairs[unit] for unit in units])
             return bank
 
         def group_y(units, bank):
             grouped = work.tile([P, 2 * BANK], BF16, name="y_grouped", tag="y_grouped", bufs=4, align_bytes=64)
             width = 2 * P * len(units)
-            nc.scalar.copy(
-                out=grouped[:].bitcast(F32)[:, 0:width].rearrange("p (s n u) -> p s n u", n=P, u=2),
-                in_=bank[:, 0:width].rearrange("p (s u n) -> p s n u", n=P, u=2),
-            )
+            group_words(grouped[:].bitcast(F32)[:, 0:width], bank[:, 0:width])
             for s, unit in enumerate(units):
                 y_grouped[unit] = grouped[:, BANK * s : BANK * (s + 1)]
 
-        def quantize_y(i, h):
+        def quantize_y(unit):
+            i, h = unit
             part = 0 if i < SCALE_SPLIT else 1
-            at = P * (i - scale_parts[part][0])
+            first, end = scale_parts[part]
             nc.vector.quantize_mx(
                 out=y_codes[h][:, P * i : P * (i + 1)].bitcast(FP8X4),
-                scales=y_scales[part][:, h, at : at + P],
-                in_=y_grouped[i, h],
+                scales=y_scales[part][:, h, P * (i - first) : P * (i - first + 1)],
+                in_=y_grouped[unit],
             )
             if i % 2 == 1:
                 m0, m1 = P * (i - 1), P * (i + 1)
@@ -273,85 +277,80 @@ def tile_photometric_sensor_render_k5_kernel(
                     out=out_1[h].rearrange("p m t -> p (m t)")[:, 4 * m0 : 4 * m1].bitcast(I32),
                     in_=y_codes[h][:, m0:m1].bitcast(I32),
                 )
-            if h == HALVES - 1 and i == scale_parts[part][1] - 1:
-                m0, m1 = P * scale_parts[part][0], P * scale_parts[part][1]
+            if unit == (end - 1, HALVES - 1):
                 for q in range(4):
-                    nc.sync.dma_start(
-                        out=out_2[:, 4 * q : 4 * q + 4, m0:m1].rearrange("h r m -> r h m").bitcast(I32),
+                    queue = nc.scalar if end == TILES and q % 2 == 0 else nc.sync
+                    queue.dma_start(
+                        out=out_2[:, 4 * q : 4 * q + 4, P * first : P * end].rearrange("h r m -> r h m").bitcast(I32),
                         in_=y_scales[part][32 * q : 32 * q + 4].bitcast(I32),
                     )
 
         def mixed_in(step):
-            return [(i, h) for i, h in ((step - 2, 0), (step - 2 - LAG, 1)) if 0 <= i]
+            units = ((step - MIX_DELAY, 0), (step - MIX_DELAY - HALF_LAG, 1))
+            return [(i, h) for i, h in units if i >= 0]
 
-        for g in range(3):
+        first_half = {0: (0, 1), 1: (2, 3)}
+        late_sides = [(1, g, side) for g in range(PASSES) for side in range(2)]
+        late_sides_in = {2: late_sides[1:4], 3: late_sides[4:7]}
+        late_passes_after = {2: (0, 1), 3: (2,)}
+
+        for g in range(PASSES - 1):
             shade_matmul(0, g)
-
         for step in range(TILES):
             mixing = mixed_in(step)
             finishing = mixed_in(step - 1)
             leaving = mixed_in(step - 2)
-            opening = step // 2 if step % 2 == 0 and step // 2 < HALVES else None
-            middle = step // 2 if step % 2 == 1 and step // 2 < HALVES else None
-            closing = step // 2 - 1 if step % 2 == 0 and 1 <= step // 2 <= HALVES else None
 
             if step >= 1:
                 turn_e(step - 1)
             if leaving:
-                y_bank = turn_y(leaving)
+                y_bank = turn_y(leaving, TURN_Y_BANKS)
             for unit in finishing:
-                fall_and_dark(*unit)
-            if closing is not None:
-                group_sensor(closing, 3, 1, "g")
-            if middle is not None:
-                group_sensor(middle, 1, 1, "g")
-            if middle == 0:
-                group_sensor(middle, 2, 1, "g")
-                group_sensor(middle, 1, 0, "s")
+                fall_and_dark(unit)
+            if step == 4:
+                group_sensor(*late_sides[-1], nc.scalar.copy)
             if step >= 1:
                 group_e(step - 1)
             if leaving:
                 group_y(leaving, y_bank)
-            if step == 2:
+            if step == 0:
                 prepare_vectors()
             for unit in finishing:
-                apply_gain(*unit)
-            if opening is not None:
-                group_sensor(opening, 0, 1, "g")
-                group_sensor(opening, 0, 0, "s")
-            if opening == 1:
-                group_sensor(opening, 1, 0, "s")
-            if middle == 1:
-                group_sensor(middle, 2, 1, "g")
-            if middle is not None:
-                group_sensor(middle, 2, 0, "s")
-                group_sensor(middle, 3, 0, "s")
+                apply_gain(unit, nc.gpsimd)
+            for g in first_half.get(step, ()):
+                group_sensor(0, g, 0, nc.scalar.copy)
+            for piece in late_sides_in.get(step, ()):
+                group_sensor(*piece, nc.scalar.copy)
             for unit in finishing:
-                round_y(*unit)
+                round_y(unit, nc.scalar.copy)
+            if step == 1:
+                group_sensor(*late_sides[0], nc.scalar.copy)
 
             if len(mixing) > 1:
-                mix_matmul(*mixing[0])
+                mix_matmul(mixing[0], Z_BANKS)
             reflect(step, 0)
-            shade_matmul(step, 3)
+            shade_matmul(step, PASSES - 1)
             reflect(step, 1)
-            if closing is not None:
-                quantize_sensor(closing, 3)
+            if step == 4:
+                quantize_sensor(1, PASSES - 1)
             if mixing:
-                mix_matmul(*mixing[-1])
+                mix_matmul(mixing[-1], Z_BANKS)
             for g in range(2, PASSES):
                 reflect(step, g)
             if step + 1 < TILES:
-                for g in range(3):
+                for g in range(PASSES - 1):
                     shade_matmul(step + 1, g)
+
+            for g in first_half.get(step, ()):
+                group_sensor(0, g, 1, nc.vector.tensor_copy)
             if step >= 1:
                 quantize_e(step - 1)
-            if opening is not None:
-                quantize_sensor(opening, 0)
-            if middle is not None:
-                quantize_sensor(middle, 1)
-                quantize_sensor(middle, 2)
+            for g in first_half.get(step, ()):
+                quantize_sensor(0, g)
+            for g in late_passes_after.get(step, ()):
+                quantize_sensor(1, g)
             for unit in leaving:
-                quantize_y(*unit)
+                quantize_y(unit)
 
         last = TILES - 1
         pairs = [mixed_in(last - 1), mixed_in(last), mixed_in(last + 1)]
@@ -359,41 +358,43 @@ def tile_photometric_sensor_render_k5_kernel(
         pairs.append([(last, 0), (last, 1)])
 
         turn_e(last)
-        y_bank = turn_y(pairs[0])
+        y_bank = turn_y(pairs[0], TURN_Y_BANKS)
         for unit in pairs[1]:
-            fall_and_dark(*unit)
+            fall_and_dark(unit)
         group_e(last)
         group_y(pairs[0], y_bank)
         for unit in pairs[1]:
-            apply_gain(*unit)
-            round_y(*unit)
+            apply_gain(unit, nc.gpsimd)
+            round_y(unit, nc.scalar.copy)
         for unit in pairs[2]:
-            mix_matmul(*unit)
+            mix_matmul(unit, Z_BANKS)
         for unit in pairs[3]:
-            mix_matmul(*unit, tag="shade", bufs=3)
+            mix_matmul(unit, SHADE_BANKS)
+
         for n in range(2, len(pairs)):
             first, second = pairs[n]
-            fall_and_dark(*first)
+            fall_and_dark(first)
             if n == 2:
                 quantize_e(last)
                 for unit in pairs[0]:
-                    quantize_y(*unit)
-            fall_and_dark(*second)
+                    quantize_y(unit)
+            fall_and_dark(second)
             for unit in pairs[n]:
-                apply_gain(*unit, engine=nc.gpsimd if n == 2 else nc.vector)
+                apply_gain(unit, nc.gpsimd if n == 2 else nc.vector)
             if n == 2:
-                mix_matmul(*pairs[-1][0], tag="shade", bufs=3)
-                y_bank = turn_y(pairs[n - 1])
-                mix_matmul(*pairs[-1][1])
+                mix_matmul(pairs[-1][0], SHADE_BANKS)
+                y_bank = turn_y(pairs[n - 1], TURN_Y_BANKS)
+                mix_matmul(pairs[-1][1], Z_BANKS)
             else:
-                y_bank = turn_y(pairs[n - 1], "turn_e", 2)
-            round_y(*first)
+                y_bank = turn_y(pairs[n - 1], TURN_E_BANKS)
+            copy = nc.vector.tensor_copy if n == len(pairs) - 1 else nc.scalar.copy
+            round_y(first, copy)
             group_y(pairs[n - 1], y_bank)
-            round_y(*second)
+            round_y(second, copy)
             if n > 2:
                 for unit in pairs[n - 2]:
-                    quantize_y(*unit)
-        for unit, tag, bufs in zip(pairs[-1], ("turn_y", "turn_e"), (1, 2)):
-            group_y([unit], turn_y([unit], tag, bufs))
+                    quantize_y(unit)
+        for unit, banks in zip(pairs[-1], (TURN_Y_BANKS, TURN_E_BANKS)):
+            group_y([unit], turn_y([unit], banks))
         for unit in pairs[-2] + pairs[-1]:
-            quantize_y(*unit)
+            quantize_y(unit)

@@ -20,6 +20,8 @@ BANK = 512
 TILES = PIXELS // P
 PASSES = LIGHTS // BANK
 HALVES = CHANNELS // BANK
+SPAN = 2 * BANK
+SPANS = LIGHTS // SPAN
 SIDE = BANK // 2
 
 MIX_DELAY = 2
@@ -45,8 +47,8 @@ def tile_photometric_sensor_render_k5_kernel(
 
         o_words = keep.tile([P, 2 * PIXELS], U8, align_bytes=64)
         o_scales = keep.tile([P, PIXELS], U8, align_bytes=64)
-        l_words = keep.tile([P, 2 * LIGHTS], U8, align_bytes=64)
-        l_scales = keep.tile([P, LIGHTS], U8, align_bytes=64)
+        l_words_in = keep.tile([P, 2 * LIGHTS], U8)
+        l_scales_in = keep.tile([P, LIGHTS], U8)
         falloff_rows = keep.tile([P, P], BF16)
         gain_cols = keep.tile([P, CHANNELS // P], BF16)
         dark_cols = keep.tile([P, CHANNELS // P], BF16)
@@ -55,7 +57,7 @@ def tile_photometric_sensor_render_k5_kernel(
         sensor_raw = {}
 
         nc.vector.memset(o_scales[:].bitcast(I32), 0)
-        nc.vector.memset(l_scales[:].bitcast(I32), 0)
+        nc.vector.memset(l_scales_in[:].bitcast(I32), 0)
         nc.vector.memset(falloff_rows[:], 0.0)
 
         def load_scale_rows(plane, rows, quadrants, queue):
@@ -75,10 +77,10 @@ def tile_photometric_sensor_render_k5_kernel(
 
         load_scale_rows(o_scales, orient_scales, (0, 1), nc.gpsimd)
         make_identity(nc, identity[:])
-        nc.sync.dma_start(out=l_words[:].bitcast(I32), in_=light_words[0].bitcast(I32))
+        nc.sync.dma_start(out=l_words_in[:].bitcast(I32), in_=light_words[0].bitcast(I32))
         nc.sync.dma_start(out=o_words[:].bitcast(I32), in_=orient_words[0].bitcast(I32))
+        load_scale_rows(l_scales_in, light_scales, range(4), nc.sync)
         load_scale_rows(o_scales, orient_scales, (2, 3), nc.sync)
-        load_scale_rows(l_scales, light_scales, range(4), nc.sync)
         load_albedo(0)
         nc.sync.dma_start(out=dark_cols[:], in_=dark.rearrange("(p j) -> p j", p=P))
         nc.sync.dma_start(out=gain_cols[:], in_=gain.rearrange("(p j) -> p j", p=P))
@@ -105,6 +107,8 @@ def tile_photometric_sensor_render_k5_kernel(
         y_scales = [
             keep.tile([P, HALVES, P * (b - a)], U8, name="y_scales_%d" % a, align_bytes=64) for a, b in scale_parts
         ]
+        l_words = [keep.tile([P, 2 * SPAN], U8, name="l_words_%d" % s, align_bytes=64) for s in range(SPANS)]
+        l_scales = [keep.tile([P, SPAN], U8, name="l_scales_%d" % s, align_bytes=64) for s in range(SPANS)]
         sensor_codes = {}
         sensor_scales = {}
         for h in range(HALVES):
@@ -145,50 +149,61 @@ def tile_photometric_sensor_render_k5_kernel(
             nc.scalar.copy(out=falloff_col[:], in_=bank[:, 0:TILES])
 
         def group_sensor(h, g, side, copy):
-            grouped = work.tile([P, 4 * SIDE], BF16, name="sensor_grouped", tag="sensor_grouped", bufs=8, align_bytes=64)
-            sensor_grouped[h, g, side] = grouped
+            if side == 0:
+                sensor_grouped[h, g] = work.tile(
+                    [P, 4 * BANK], BF16, name="sensor_grouped", tag="sensor_grouped", bufs=4, align_bytes=64
+                )
             copy(
-                out=grouped[:].rearrange("p (c i t) -> p c t i", i=4, t=4),
+                out=sensor_grouped[h, g][:, 4 * SIDE * side : 4 * SIDE * (side + 1)].rearrange("p (c i t) -> p c t i", i=4, t=4),
                 in_=sensor_raw[h, g][:, :, SIDE * side : SIDE * (side + 1)].rearrange("p t (c i) -> p c t i", i=4),
             )
 
         def quantize_sensor(h, g):
-            for side in range(2):
-                cols = slice(SIDE * side, SIDE * (side + 1))
-                nc.vector.quantize_mx(
-                    out=sensor_codes[h, g][:, cols].bitcast(FP8X4),
-                    scales=sensor_scales[h, g][:, cols],
-                    in_=sensor_grouped[h, g, side][:],
-                )
+            nc.vector.quantize_mx(
+                out=sensor_codes[h, g][:].bitcast(FP8X4), scales=sensor_scales[h, g][:], in_=sensor_grouped[h, g][:]
+            )
 
-        def shade_matmul(i, g):
-            shade[i, g] = psum.tile([P, BANK], F32, name="shade", **SHADE_BANKS)
+        def sort_light_words(s):
+            nc.vector.tensor_copy(
+                out=l_words[s][:].bitcast(I32).rearrange("p (u q) -> p u q", u=2),
+                in_=l_words_in[:, 2 * SPAN * s : 2 * SPAN * (s + 1)].bitcast(I32).rearrange("p (q u) -> p u q", u=2),
+            )
+
+        def sort_light_scales(s):
+            nc.vector.tensor_copy(
+                out=l_scales[s][:].rearrange("p (u q e) -> p u q e", u=2, e=2),
+                in_=l_scales_in[:, SPAN * s : SPAN * (s + 1)].rearrange("p (q u e) -> p u q e", u=2, e=2),
+            )
+
+        def shade_matmul(i, b):
+            s, u = divmod(b, 2)
+            shade[i, b] = psum.tile([P, BANK], F32, name="shade", **SHADE_BANKS)
             nc.tensor.matmul_mx(
-                out=shade[i, g][:],
+                out=shade[i, b][:],
                 lhsT=o_words[:, 2 * P * i : 2 * P * (i + 1)].bitcast(FP4X4),
                 lhsT_scale=o_scales[:, P * i : P * (i + 1)],
-                rhs=l_words[:, 2 * BANK * g : 2 * BANK * (g + 1)].bitcast(FP4X4),
-                rhs_scale=l_scales[:, BANK * g : BANK * (g + 1)],
+                rhs=l_words[s][:, 2 * BANK * u : 2 * BANK * (u + 1)].bitcast(FP4X4),
+                rhs_scale=l_scales[s][:, BANK * u : BANK * (u + 1)],
                 start=True,
                 stop=True,
             )
 
-        def reflect(i, g):
-            e_pairs[i, g] = work.tile([P, BANK], BF16, name="e_pairs", tag="e_pairs", bufs=2 * PASSES)
-            shade_v = shade[i, g][:].rearrange("n (p u e) -> n u p e", u=2, e=2)
-            albedo_v = albedo_sb[i][:, BANK * g : BANK * (g + 1)].rearrange("n (p u e) -> n u p e", u=2, e=2)
-            e_v = e_pairs[i, g][:].rearrange("n (u p e) -> n u p e", u=2, e=2)
-            for u in range(2):
-                nc.vector.scalar_tensor_tensor(
-                    out=e_v[:, u], in0=shade_v[:, u], scalar=0.0, in1=albedo_v[:, u], op0=ALU.max, op1=ALU.mult
-                )
+        def reflect(i, b):
+            s, u = divmod(b, 2)
+            e_pairs[i, b] = work.tile([P, BANK], BF16, name="e_pairs", tag="e_pairs", bufs=2 * PASSES)
+            albedo_v = albedo_sb[i][:, SPAN * s : SPAN * (s + 1)].rearrange("n (q u e) -> n u q e", u=2, e=2)
+            nc.vector.scalar_tensor_tensor(
+                out=e_pairs[i, b][:].rearrange("n (q e) -> n q e", e=2),
+                in0=shade[i, b][:].rearrange("n (q e) -> n q e", e=2),
+                scalar=0.0, in1=albedo_v[:, u], op0=ALU.max, op1=ALU.mult,
+            )
 
-        def turn_words(bank, sources):
-            for s, source in enumerate(sources):
-                words = source[:].bitcast(F32)
-                for u in range(2):
-                    at = P * (2 * s + u)
-                    nc.tensor.transpose(bank[:, at : at + P], words[:, P * u : P * (u + 1)], identity[:])
+        def turn_words(bank, runs):
+            for quarter, run in enumerate(runs):
+                nc.tensor.transpose(bank[:, P * quarter : P * (quarter + 1)], run, identity[:])
+
+        def word_run(pairs_tile, n):
+            return pairs_tile[:].bitcast(F32)[:, P * n : P * (n + 1)]
 
         def group_words(words, bank):
             nc.scalar.copy(
@@ -197,15 +212,15 @@ def tile_photometric_sensor_render_k5_kernel(
             )
 
         def turn_e(i):
-            for pair in range(PASSES // 2):
-                e_turned[i, pair] = psum.tile([P, BANK], F32, name="e_turned", **TURN_E_BANKS)
-                turn_words(e_turned[i, pair], [e_pairs[i, 2 * pair], e_pairs[i, 2 * pair + 1]])
+            for s in range(SPANS):
+                e_turned[i, s] = psum.tile([P, BANK], F32, name="e_turned", **TURN_E_BANKS)
+                turn_words(e_turned[i, s], [word_run(e_pairs[i, 2 * s + u], n) for n in range(2) for u in range(2)])
 
         def group_e(i):
             e_grouped[i] = work.tile([P, LIGHTS], BF16, name="e_grouped", tag="e_grouped", bufs=2, align_bytes=64)
             words = e_grouped[i][:].bitcast(F32)
-            for pair in range(PASSES // 2):
-                group_words(words[:, BANK * pair : BANK * (pair + 1)], e_turned[i, pair][:])
+            for s in range(SPANS):
+                group_words(words[:, BANK * s : BANK * (s + 1)], e_turned[i, s][:])
 
         def quantize_e(i):
             bufs = HALF_LAG + 3
@@ -252,7 +267,7 @@ def tile_photometric_sensor_render_k5_kernel(
 
         def turn_y(units, banks):
             bank = psum.tile([P, BANK], F32, name="y_turned", **banks)
-            turn_words(bank, [y_pairs[unit] for unit in units])
+            turn_words(bank, [word_run(y_pairs[unit], u) for unit in units for u in range(2)])
             return bank
 
         def group_y(units, bank):
@@ -294,8 +309,12 @@ def tile_photometric_sensor_render_k5_kernel(
         late_sides_in = {2: late_sides[1:4], 3: late_sides[4:7]}
         late_passes_after = {2: (0, 1), 3: (2,)}
 
-        for g in range(PASSES - 1):
-            shade_matmul(0, g)
+        for s in range(SPANS):
+            sort_light_words(s)
+        for s in range(SPANS):
+            sort_light_scales(s)
+        for b in range(PASSES - 1):
+            shade_matmul(0, b)
         for step in range(TILES):
             mixing = mixed_in(step)
             finishing = mixed_in(step - 1)
@@ -335,11 +354,11 @@ def tile_photometric_sensor_render_k5_kernel(
                 quantize_sensor(1, PASSES - 1)
             if mixing:
                 mix_matmul(mixing[-1], Z_BANKS)
-            for g in range(2, PASSES):
-                reflect(step, g)
+            for b in range(2, PASSES):
+                reflect(step, b)
             if step + 1 < TILES:
-                for g in range(PASSES - 1):
-                    shade_matmul(step + 1, g)
+                for b in range(PASSES - 1):
+                    shade_matmul(step + 1, b)
 
             for g in first_half.get(step, ()):
                 group_sensor(0, g, 1, nc.vector.tensor_copy)

@@ -56,9 +56,9 @@ def tile_photometric_sensor_render_k5_kernel(
         albedo_sb = {}
         sensor_raw = {}
 
-        nc.vector.memset(o_scales[:].bitcast(I32), 0)
         nc.vector.memset(l_scales_in[:].bitcast(I32), 0)
         nc.vector.memset(falloff_rows[:], 0.0)
+        nc.vector.memset(o_scales[:].bitcast(I32), 0)
 
         def load_scale_rows(plane, rows, quadrants, queue):
             for q in quadrants:
@@ -75,16 +75,15 @@ def tile_photometric_sensor_render_k5_kernel(
             rows = sensor[BANK * g : BANK * (g + 1), BANK * h : BANK * (h + 1)]
             nc.sync.dma_start(out=sensor_raw[h, g][:], in_=rows.rearrange("(p t) c -> p t c", t=4))
 
-        load_scale_rows(o_scales, orient_scales, (0, 1), nc.gpsimd)
+        nc.scalar.dma_start(out=dark_cols[:], in_=dark.rearrange("(p j) -> p j", p=P))
+        nc.scalar.dma_start(out=gain_cols[:], in_=gain.rearrange("(p j) -> p j", p=P))
+        nc.scalar.dma_start(out=falloff_rows[0:TILES, :], in_=falloff.rearrange("(i p) -> i p", p=P))
         make_identity(nc, identity[:])
         nc.sync.dma_start(out=l_words_in[:].bitcast(I32), in_=light_words[0].bitcast(I32))
         nc.sync.dma_start(out=o_words[:].bitcast(I32), in_=orient_words[0].bitcast(I32))
         load_scale_rows(l_scales_in, light_scales, range(4), nc.sync)
-        load_scale_rows(o_scales, orient_scales, (2, 3), nc.sync)
         load_albedo(0)
-        nc.sync.dma_start(out=dark_cols[:], in_=dark.rearrange("(p j) -> p j", p=P))
-        nc.sync.dma_start(out=gain_cols[:], in_=gain.rearrange("(p j) -> p j", p=P))
-        nc.sync.dma_start(out=falloff_rows[0:TILES, :], in_=falloff.rearrange("(i p) -> i p", p=P))
+        load_scale_rows(o_scales, orient_scales, range(4), nc.sync)
         load_sensor(0, 0)
         load_sensor(0, 1)
         load_albedo(1)
@@ -148,14 +147,26 @@ def tile_photometric_sensor_render_k5_kernel(
             nc.tensor.transpose(bank[:, 0:P], falloff_f32[:], identity[:])
             nc.scalar.copy(out=falloff_col[:], in_=bank[:, 0:TILES])
 
-        def group_sensor(h, g, side, copy):
-            if side == 0:
+        def sensor_side(h, g, side):
+            if (h, g) not in sensor_grouped:
                 sensor_grouped[h, g] = work.tile(
                     [P, 4 * BANK], BF16, name="sensor_grouped", tag="sensor_grouped", bufs=4, align_bytes=64
                 )
+            raw = sensor_raw[h, g][:, :, SIDE * side : SIDE * (side + 1)]
+            return raw, sensor_grouped[h, g][:, 4 * SIDE * side : 4 * SIDE * (side + 1)]
+
+        def group_sensor(h, g, side, copy):
+            raw, grouped = sensor_side(h, g, side)
             copy(
-                out=sensor_grouped[h, g][:, 4 * SIDE * side : 4 * SIDE * (side + 1)].rearrange("p (c i t) -> p c t i", i=4, t=4),
-                in_=sensor_raw[h, g][:, :, SIDE * side : SIDE * (side + 1)].rearrange("p t (c i) -> p c t i", i=4),
+                out=grouped.rearrange("p (c i t) -> p c t i", i=4, t=4),
+                in_=raw.rearrange("p t (c i) -> p c t i", i=4),
+            )
+
+        def group_sensor_gpsimd(h, g, side):
+            raw, grouped = sensor_side(h, g, side)
+            nc.gpsimd.tensor_scalar(
+                out=grouped.rearrange("p (c t) -> p c t", t=4), in0=raw.rearrange("p t c -> p c t"),
+                scalar1=1.0, scalar2=0.0, op0=ALU.mult, op1=ALU.add,
             )
 
         def quantize_sensor(h, g):
@@ -304,11 +315,10 @@ def tile_photometric_sensor_render_k5_kernel(
             units = ((step - MIX_DELAY, 0), (step - MIX_DELAY - HALF_LAG, 1))
             return [(i, h) for i, h in units if i >= 0]
 
-        first_half = {0: (0, 1), 1: (2, 3)}
-        late_sides = [(1, g, side) for g in range(PASSES) for side in range(2)]
-        late_sides_in = {2: late_sides[1:4], 3: late_sides[4:7]}
-        late_passes_after = {2: (0, 1), 3: (2,)}
+        pieces = [(h, g) for h in range(HALVES) for g in range(PASSES)]
+        sensor_steps = len(pieces) // 2
 
+        prepare_vectors()
         for s in range(SPANS):
             sort_light_words(s)
         for s in range(SPANS):
@@ -319,6 +329,10 @@ def tile_photometric_sensor_render_k5_kernel(
             mixing = mixed_in(step)
             finishing = mixed_in(step - 1)
             leaving = mixed_in(step - 2)
+            preparing = step < sensor_steps
+            if preparing:
+                even, odd = pieces[2 * step : 2 * step + 2]
+                first_half = even[0] == 0
 
             if step >= 1:
                 turn_e(step - 1)
@@ -326,32 +340,29 @@ def tile_photometric_sensor_render_k5_kernel(
                 y_bank = turn_y(leaving, TURN_Y_BANKS)
             for unit in finishing:
                 fall_and_dark(unit)
-            if step == 4:
-                group_sensor(*late_sides[-1], nc.scalar.copy)
             if step >= 1:
                 group_e(step - 1)
             if leaving:
                 group_y(leaving, y_bank)
-            if step == 0:
-                prepare_vectors()
             for unit in finishing:
                 apply_gain(unit, nc.gpsimd)
-            for g in first_half.get(step, ()):
-                group_sensor(0, g, 0, nc.scalar.copy)
-            for piece in late_sides_in.get(step, ()):
-                group_sensor(*piece, nc.scalar.copy)
+            if preparing:
+                group_sensor_gpsimd(*even, 1)
+                if first_half:
+                    group_sensor(*even, 0, nc.scalar.copy)
+                group_sensor(*odd, 0, nc.scalar.copy)
+                if not first_half:
+                    group_sensor(*odd, 1, nc.scalar.copy)
             for unit in finishing:
                 round_y(unit, nc.scalar.copy)
-            if step == 1:
-                group_sensor(*late_sides[0], nc.scalar.copy)
+            if step + 1 < sensor_steps and pieces[2 * step + 2][0] == 1:
+                group_sensor(*pieces[2 * step + 2], 0, nc.scalar.copy)
 
             if len(mixing) > 1:
                 mix_matmul(mixing[0], Z_BANKS)
             reflect(step, 0)
             shade_matmul(step, PASSES - 1)
             reflect(step, 1)
-            if step == 4:
-                quantize_sensor(1, PASSES - 1)
             if mixing:
                 mix_matmul(mixing[-1], Z_BANKS)
             for b in range(2, PASSES):
@@ -360,14 +371,13 @@ def tile_photometric_sensor_render_k5_kernel(
                 for b in range(PASSES - 1):
                     shade_matmul(step + 1, b)
 
-            for g in first_half.get(step, ()):
-                group_sensor(0, g, 1, nc.vector.tensor_copy)
+            if preparing and first_half:
+                group_sensor(*odd, 1, nc.vector.tensor_copy)
             if step >= 1:
                 quantize_e(step - 1)
-            for g in first_half.get(step, ()):
-                quantize_sensor(0, g)
-            for g in late_passes_after.get(step, ()):
-                quantize_sensor(1, g)
+            if preparing:
+                quantize_sensor(*even)
+                quantize_sensor(*odd)
             for unit in leaving:
                 quantize_y(unit)
 

from contextlib import ExitStack

import concourse.mybir as mybir
from concourse.masks import make_identity

PIXELS, CODE, LIGHTS, CHANNELS = 1536, 512, 2048, 1024
FLOPS = 2 * PIXELS * LIGHTS * CODE + 2 * PIXELS * CHANNELS * LIGHTS

F32 = mybir.dt.float32
BF16 = mybir.dt.bfloat16
I32 = mybir.dt.int32
U32 = mybir.dt.uint32
U8 = mybir.dt.uint8
FP8X4 = mybir.dt.float8_e4m3fn_x4
FP4X4 = mybir.dt.float4_e2m1fn_x4
ALU = mybir.AluOpType

P = 128
BANK = 512
TILES = PIXELS // P
PASSES = LIGHTS // BANK
HALVES = CHANNELS // BANK
SPAN = 2 * BANK
SPANS = LIGHTS // SPAN
SIDE = BANK // 2

MIX_DELAY = 2
HALF_LAG = 2
SCALE_SPLIT = 6

SHADE_BANKS = {"tag": "shade", "bufs": 3}
Z_BANKS = {"tag": "z", "bufs": 2}
TURN_E_BANKS = {"tag": "turn_e", "bufs": 2}
TURN_Y_BANKS = {"tag": "turn_y", "bufs": 1}


def tile_photometric_sensor_render_k5_kernel(
    tc, orient_words, orient_scales, light_words, light_scales, albedo, sensor, falloff, dark, gain,
    out_0, out_1, out_2,
):
    nc = tc.nc
    with ExitStack() as ctx:
        keep = ctx.enter_context(tc.tile_pool(name="keep", bufs=1))
        work = ctx.enter_context(tc.tile_pool(name="work", bufs=2))
        psum = ctx.enter_context(tc.psum_pool(name="psum", bufs=1))
        ctx.enter_context(tc.manual_schedule())

        o_words = keep.tile([P, 2 * PIXELS], U8, align_bytes=64)
        o_scales = keep.tile([P, PIXELS], U8, align_bytes=64)
        l_words_in = keep.tile([P, 2 * LIGHTS], U8)
        l_scales_in = keep.tile([P, LIGHTS], U8)
        falloff_rows = keep.tile([P, P], BF16)
        gain_cols = keep.tile([P, CHANNELS // P], BF16)
        dark_cols = keep.tile([P, CHANNELS // P], BF16)
        identity = keep.tile([P, P], F32)
        albedo_sb = {}
        sensor_raw = {}

        nc.vector.memset(l_scales_in[:].bitcast(I32), 0)
        nc.vector.memset(falloff_rows[:], 0.0)
        nc.vector.memset(o_scales[:].bitcast(I32), 0)

        def load_scale_rows(plane, rows, quadrants, queue):
            for q in quadrants:
                queue.dma_start(
                    out=plane[32 * q : 32 * q + 4, :].bitcast(I32), in_=rows[0, 4 * q : 4 * q + 4, :].bitcast(I32)
                )

        def load_albedo(i):
            albedo_sb[i] = keep.tile([P, LIGHTS], BF16, name="albedo_%d" % i)
            nc.sync.dma_start(out=albedo_sb[i][:], in_=albedo[P * i : P * (i + 1), :])

        def load_sensor(h, g):
            sensor_raw[h, g] = keep.tile([P, 4, BANK], BF16, name="sensor_raw_%d_%d" % (h, g))
            rows = sensor[BANK * g : BANK * (g + 1), BANK * h : BANK * (h + 1)]
            nc.sync.dma_start(out=sensor_raw[h, g][:], in_=rows.rearrange("(p t) c -> p t c", t=4))

        nc.scalar.dma_start(out=dark_cols[:], in_=dark.rearrange("(p j) -> p j", p=P))
        nc.scalar.dma_start(out=gain_cols[:], in_=gain.rearrange("(p j) -> p j", p=P))
        nc.scalar.dma_start(out=falloff_rows[0:TILES, :], in_=falloff.rearrange("(i p) -> i p", p=P))
        make_identity(nc, identity[:])
        nc.sync.dma_start(out=l_words_in[:].bitcast(I32), in_=light_words[0].bitcast(I32))
        nc.sync.dma_start(out=o_words[:].bitcast(I32), in_=orient_words[0].bitcast(I32))
        load_scale_rows(l_scales_in, light_scales, range(4), nc.sync)
        load_albedo(0)
        load_scale_rows(o_scales, orient_scales, range(4), nc.sync)
        load_sensor(0, 0)
        load_sensor(0, 1)
        load_albedo(1)
        load_sensor(0, 2)
        load_sensor(0, 3)
        load_sensor(1, 0)
        load_albedo(2)
        load_sensor(1, 1)
        load_albedo(3)
        load_sensor(1, 2)
        load_sensor(1, 3)
        for i in range(4, TILES):
            load_albedo(i)

        falloff_col = keep.tile([P, TILES], F32)
        gain_all = keep.tile([P, CHANNELS], BF16)
        dark_all = keep.tile([P, CHANNELS], BF16)
        y_codes = [keep.tile([P, PIXELS], U32, name="y_codes_%d" % h, align_bytes=64) for h in range(HALVES)]
        scale_parts = [(0, SCALE_SPLIT), (SCALE_SPLIT, TILES)]
        y_scales = [
            keep.tile([P, HALVES, P * (b - a)], U8, name="y_scales_%d" % a, align_bytes=64) for a, b in scale_parts
        ]
        l_words = [keep.tile([P, 2 * SPAN], U8, name="l_words_%d" % s, align_bytes=64) for s in range(SPANS)]
        l_scales = [keep.tile([P, SPAN], U8, name="l_scales_%d" % s, align_bytes=64) for s in range(SPANS)]
        sensor_codes = {}
        sensor_scales = {}
        for h in range(HALVES):
            for g in range(PASSES):
                sensor_codes[h, g] = keep.tile([P, BANK], U32, name="sensor_codes_%d_%d" % (h, g), align_bytes=64)
                sensor_scales[h, g] = keep.tile([P, BANK], U8, name="sensor_scales_%d_%d" % (h, g), align_bytes=64)

        sensor_grouped = {}
        shade = {}
        e_pairs = {}
        e_turned = {}
        e_grouped = {}
        e_codes = {}
        e_scales = {}
        z = {}
        inner = {}
        y = {}
        y_pairs = {}
        y_grouped = {}

        def spread_vector(cols, spread):
            bank = psum.tile([P, BANK], F32, name="spread_bank", **Z_BANKS)
            words = cols[:].bitcast(F32)
            for j in range(4):
                nc.tensor.transpose(bank[:, P * j : P * (j + 1)], words[:, j : j + 1].to_broadcast([P, P]), identity[:])
            nc.scalar.copy(
                out=spread[:].bitcast(F32).rearrange("q (p j) -> q p j", j=4),
                in_=bank[:].rearrange("q (j p) -> q p j", j=4),
            )

        def prepare_vectors():
            falloff_f32 = keep.tile([P, P], F32)
            nc.scalar.copy(out=falloff_f32[:], in_=falloff_rows[:])
            spread_vector(dark_cols, dark_all)
            spread_vector(gain_cols, gain_all)
            bank = psum.tile([P, BANK], F32, name="falloff_bank", **TURN_Y_BANKS)
            nc.tensor.transpose(bank[:, 0:P], falloff_f32[:], identity[:])
            nc.scalar.copy(out=falloff_col[:], in_=bank[:, 0:TILES])

        def sensor_side(h, g, side):
            if (h, g) not in sensor_grouped:
                sensor_grouped[h, g] = work.tile(
                    [P, 4 * BANK], BF16, name="sensor_grouped", tag="sensor_grouped", bufs=4, align_bytes=64
                )
            raw = sensor_raw[h, g][:, :, SIDE * side : SIDE * (side + 1)]
            return raw, sensor_grouped[h, g][:, 4 * SIDE * side : 4 * SIDE * (side + 1)]

        def group_sensor(h, g, side, copy):
            raw, grouped = sensor_side(h, g, side)
            copy(
                out=grouped.rearrange("p (c i t) -> p c t i", i=4, t=4),
                in_=raw.rearrange("p t (c i) -> p c t i", i=4),
            )

        def group_sensor_gpsimd(h, g, side):
            raw, grouped = sensor_side(h, g, side)
            nc.gpsimd.tensor_scalar(
                out=grouped.rearrange("p (c t) -> p c t", t=4), in0=raw.rearrange("p t c -> p c t"),
                scalar1=1.0, scalar2=0.0, op0=ALU.mult, op1=ALU.add,
            )

        def quantize_sensor(h, g):
            nc.vector.quantize_mx(
                out=sensor_codes[h, g][:].bitcast(FP8X4), scales=sensor_scales[h, g][:], in_=sensor_grouped[h, g][:]
            )

        def sort_light_words(s):
            nc.vector.tensor_copy(
                out=l_words[s][:].bitcast(I32).rearrange("p (u q) -> p u q", u=2),
                in_=l_words_in[:, 2 * SPAN * s : 2 * SPAN * (s + 1)].bitcast(I32).rearrange("p (q u) -> p u q", u=2),
            )

        def sort_light_scales(s):
            nc.vector.tensor_copy(
                out=l_scales[s][:].rearrange("p (u q e) -> p u q e", u=2, e=2),
                in_=l_scales_in[:, SPAN * s : SPAN * (s + 1)].rearrange("p (q u e) -> p u q e", u=2, e=2),
            )

        def shade_matmul(i, b):
            s, u = divmod(b, 2)
            shade[i, b] = psum.tile([P, BANK], F32, name="shade", **SHADE_BANKS)
            nc.tensor.matmul_mx(
                out=shade[i, b][:],
                lhsT=o_words[:, 2 * P * i : 2 * P * (i + 1)].bitcast(FP4X4),
                lhsT_scale=o_scales[:, P * i : P * (i + 1)],
                rhs=l_words[s][:, 2 * BANK * u : 2 * BANK * (u + 1)].bitcast(FP4X4),
                rhs_scale=l_scales[s][:, BANK * u : BANK * (u + 1)],
                start=True,
                stop=True,
            )

        def reflect(i, b):
            s, u = divmod(b, 2)
            e_pairs[i, b] = work.tile([P, BANK], BF16, name="e_pairs", tag="e_pairs", bufs=2 * PASSES)
            albedo_v = albedo_sb[i][:, SPAN * s : SPAN * (s + 1)].rearrange("n (q u e) -> n u q e", u=2, e=2)
            nc.vector.scalar_tensor_tensor(
                out=e_pairs[i, b][:].rearrange("n (q e) -> n q e", e=2),
                in0=shade[i, b][:].rearrange("n (q e) -> n q e", e=2),
                scalar=0.0, in1=albedo_v[:, u], op0=ALU.max, op1=ALU.mult,
            )

        def turn_words(bank, runs):
            for quarter, run in enumerate(runs):
                nc.tensor.transpose(bank[:, P * quarter : P * (quarter + 1)], run, identity[:])

        def word_run(pairs_tile, n):
            return pairs_tile[:].bitcast(F32)[:, P * n : P * (n + 1)]

        def group_words(words, bank):
            nc.scalar.copy(
                out=words.rearrange("p (s n u) -> p s n u", n=P, u=2),
                in_=bank.rearrange("p (s u n) -> p s n u", n=P, u=2),
            )

        def turn_e(i):
            for s in range(SPANS):
                e_turned[i, s] = psum.tile([P, BANK], F32, name="e_turned", **TURN_E_BANKS)
                turn_words(e_turned[i, s], [word_run(e_pairs[i, 2 * s + u], n) for n in range(2) for u in range(2)])

        def group_e(i):
            e_grouped[i] = work.tile([P, LIGHTS], BF16, name="e_grouped", tag="e_grouped", bufs=2, align_bytes=64)
            words = e_grouped[i][:].bitcast(F32)
            for s in range(SPANS):
                group_words(words[:, BANK * s : BANK * (s + 1)], e_turned[i, s][:])

        def quantize_e(i):
            bufs = HALF_LAG + 3
            e_codes[i] = work.tile([P, PASSES * P], U32, name="e_codes", tag="e_codes", bufs=bufs, align_bytes=64)
            e_scales[i] = work.tile([P, PASSES * P], U8, name="e_scales", tag="e_scales", bufs=bufs, align_bytes=64)
            nc.vector.quantize_mx(out=e_codes[i][:].bitcast(FP8X4), scales=e_scales[i][:], in_=e_grouped[i][:])

        def mix_matmul(unit, banks):
            i, h = unit
            z[unit] = psum.tile([P, BANK], F32, name="z", **banks)
            for g in range(PASSES):
                nc.tensor.matmul_mx(
                    out=z[unit][:],
                    lhsT=e_codes[i][:, P * g : P * (g + 1)].bitcast(FP8X4),
                    lhsT_scale=e_scales[i][:, P * g : P * (g + 1)],
                    rhs=sensor_codes[h, g][:].bitcast(FP8X4),
                    rhs_scale=sensor_scales[h, g][:],
                    start=(g == 0),
                    stop=(g == PASSES - 1),
                )

        def fall_and_dark(unit):
            i, h = unit
            inner[unit] = work.tile([P, BANK], F32, name="inner", tag="inner", bufs=6)
            nc.vector.scalar_tensor_tensor(
                out=inner[unit][:], in0=z[unit][:], scalar=falloff_col[:, i : i + 1],
                in1=dark_all[:, BANK * h : BANK * (h + 1)], op0=ALU.mult, op1=ALU.add,
            )

        def apply_gain(unit, engine):
            i, h = unit
            y[unit] = work.tile([P, BANK], F32, name="y", tag="y", bufs=10)
            engine.tensor_tensor(
                out=y[unit][:], in0=inner[unit][:], in1=gain_all[:, BANK * h : BANK * (h + 1)], op=ALU.mult
            )
            nc.sync.dma_start(out=out_0[P * i : P * (i + 1), BANK * h : BANK * (h + 1)], in_=y[unit][:])

        def round_y(unit, copy):
            y_pairs[unit] = work.tile([P, BANK], BF16, name="y_pairs", tag="y_pairs", bufs=6)
            copy(
                out=y_pairs[unit][:].rearrange("n (u p e) -> n u p e", u=2, e=2),
                in_=y[unit][:].rearrange("n (p u e) -> n u p e", u=2, e=2),
            )

        def turn_y(units, banks):
            bank = psum.tile([P, BANK], F32, name="y_turned", **banks)
            turn_words(bank, [word_run(y_pairs[unit], u) for unit in units for u in range(2)])
            return bank

        def group_y(units, bank):
            grouped = work.tile([P, 2 * BANK], BF16, name="y_grouped", tag="y_grouped", bufs=4, align_bytes=64)
            width = 2 * P * len(units)
            group_words(grouped[:].bitcast(F32)[:, 0:width], bank[:, 0:width])
            for s, unit in enumerate(units):
                y_grouped[unit] = grouped[:, BANK * s : BANK * (s + 1)]

        def quantize_y(unit):
            i, h = unit
            part = 0 if i < SCALE_SPLIT else 1
            first, end = scale_parts[part]
            nc.vector.quantize_mx(
                out=y_codes[h][:, P * i : P * (i + 1)].bitcast(FP8X4),
                scales=y_scales[part][:, h, P * (i - first) : P * (i - first + 1)],
                in_=y_grouped[unit],
            )
            if i % 2 == 1:
                m0, m1 = P * (i - 1), P * (i + 1)
                nc.sync.dma_start(
                    out=out_1[h].rearrange("p m t -> p (m t)")[:, 4 * m0 : 4 * m1].bitcast(I32),
                    in_=y_codes[h][:, m0:m1].bitcast(I32),
                )
            if unit == (end - 1, HALVES - 1):
                for q in range(4):
                    queue = nc.scalar if end == TILES and q % 2 == 0 else nc.sync
                    queue.dma_start(
                        out=out_2[:, 4 * q : 4 * q + 4, P * first : P * end].rearrange("h r m -> r h m").bitcast(I32),
                        in_=y_scales[part][32 * q : 32 * q + 4].bitcast(I32),
                    )

        def mixed_in(step):
            units = ((step - MIX_DELAY, 0), (step - MIX_DELAY - HALF_LAG, 1))
            return [(i, h) for i, h in units if i >= 0]

        pieces = [(h, g) for h in range(HALVES) for g in range(PASSES)]
        sensor_steps = len(pieces) // 2

        prepare_vectors()
        for s in range(SPANS):
            sort_light_words(s)
        for s in range(SPANS):
            sort_light_scales(s)
        for b in range(PASSES - 1):
            shade_matmul(0, b)
        for step in range(TILES):
            mixing = mixed_in(step)
            finishing = mixed_in(step - 1)
            leaving = mixed_in(step - 2)
            preparing = step < sensor_steps
            if preparing:
                even, odd = pieces[2 * step : 2 * step + 2]
                first_half = even[0] == 0

            if step >= 1:
                turn_e(step - 1)
            if leaving:
                y_bank = turn_y(leaving, TURN_Y_BANKS)
            for unit in finishing:
                fall_and_dark(unit)
            if step >= 1:
                group_e(step - 1)
            if leaving:
                group_y(leaving, y_bank)
            for unit in finishing:
                apply_gain(unit, nc.gpsimd)
            if preparing:
                group_sensor_gpsimd(*even, 1)
                if first_half:
                    group_sensor(*even, 0, nc.scalar.copy)
                group_sensor(*odd, 0, nc.scalar.copy)
                if not first_half:
                    group_sensor(*odd, 1, nc.scalar.copy)
            for unit in finishing:
                round_y(unit, nc.scalar.copy)
            if step + 1 < sensor_steps and pieces[2 * step + 2][0] == 1:
                group_sensor(*pieces[2 * step + 2], 0, nc.scalar.copy)

            if len(mixing) > 1:
                mix_matmul(mixing[0], Z_BANKS)
            reflect(step, 0)
            shade_matmul(step, PASSES - 1)
            reflect(step, 1)
            if mixing:
                mix_matmul(mixing[-1], Z_BANKS)
            for b in range(2, PASSES):
                reflect(step, b)
            if step + 1 < TILES:
                for b in range(PASSES - 1):
                    shade_matmul(step + 1, b)

            if preparing and first_half:
                group_sensor(*odd, 1, nc.vector.tensor_copy)
            if step >= 1:
                quantize_e(step - 1)
            if preparing:
                quantize_sensor(*even)
                quantize_sensor(*odd)
            for unit in leaving:
                quantize_y(unit)

        last = TILES - 1
        pairs = [mixed_in(last - 1), mixed_in(last), mixed_in(last + 1)]
        pairs.append([(last - 2, 1), (last - 1, 1)])
        pairs.append([(last, 0), (last, 1)])

        turn_e(last)
        y_bank = turn_y(pairs[0], TURN_Y_BANKS)
        for unit in pairs[1]:
            fall_and_dark(unit)
        group_e(last)
        group_y(pairs[0], y_bank)
        for unit in pairs[1]:
            apply_gain(unit, nc.gpsimd)
            round_y(unit, nc.scalar.copy)
        for unit in pairs[2]:
            mix_matmul(unit, Z_BANKS)
        for unit in pairs[3]:
            mix_matmul(unit, SHADE_BANKS)

        for n in range(2, len(pairs)):
            first, second = pairs[n]
            fall_and_dark(first)
            if n == 2:
                quantize_e(last)
                for unit in pairs[0]:
                    quantize_y(unit)
            fall_and_dark(second)
            for unit in pairs[n]:
                apply_gain(unit, nc.gpsimd if n == 2 else nc.vector)
            if n == 2:
                mix_matmul(pairs[-1][0], SHADE_BANKS)
                y_bank = turn_y(pairs[n - 1], TURN_Y_BANKS)
                mix_matmul(pairs[-1][1], Z_BANKS)
            else:
                y_bank = turn_y(pairs[n - 1], TURN_E_BANKS)
            copy = nc.vector.tensor_copy if n == len(pairs) - 1 else nc.scalar.copy
            round_y(first, copy)
            group_y(pairs[n - 1], y_bank)
            round_y(second, copy)
            if n > 2:
                for unit in pairs[n - 2]:
                    quantize_y(unit)
        for unit, banks in zip(pairs[-1], (TURN_Y_BANKS, TURN_E_BANKS)):
            group_y([unit], turn_y([unit], banks))
        for unit in pairs[-2] + pairs[-1]:
            quantize_y(unit)
